import numpy as np
import ml_dtypes


def mxq(x, axis, fmt="e4m3"):
    dtype, down = {"e4m3": (ml_dtypes.float8_e4m3fn, 7), "e5m2": (ml_dtypes.float8_e5m2, 14)}[fmt]
    v = np.moveaxis(np.asarray(x, np.float32).astype(ml_dtypes.bfloat16).astype(np.float64), axis, -1)
    blocks = v.reshape(v.shape[:-1] + (-1, 32))
    amax = np.abs(blocks).max(-1, keepdims=True)
    byte = np.maximum(np.where(amax > 0, np.frexp(amax)[1] - 1 + 127, 0) - down, 1)
    scale = np.exp2(byte - 127.0)
    codes = (blocks / scale).astype(np.float32).astype(dtype).astype(np.float64)
    return np.moveaxis((codes * scale).reshape(v.shape), -1, axis)


WIDE = False


def mx_kscale(k):
    if not WIDE:
        return np.ones(k)
    levels = np.array([10, -10, 5, -5, 0])
    if k % 512:
        return np.exp2(np.random.permutation(np.resize(levels, k // 32))).repeat(32)
    a = np.empty((k // 512, 16))
    for p in range(k // 512):
        a[p, :8] = np.random.permutation(np.resize(levels, 8))
        for g in range(8):
            far = levels[np.abs(levels - a[p, g]) >= 10]
            a[p, g + 8] = far[np.random.randint(len(far))]
    return np.exp2(a.ravel()).repeat(32)


def f64(x):
    return np.asarray(x).astype(np.float64)


def striped(idx):
    return np.tile(idx.reshape(-1, 16).T, (8, 1)).astype(np.uint16)


def unstriped(offs):
    return offs[:16].T.reshape(-1).astype(np.int64)


E2M1 = np.array([0.0, 0.5, 1.0, 1.5, 2.0, 3.0, 4.0, 6.0, -0.0, -0.5, -1.0, -1.5, -2.0, -3.0, -4.0, -6.0])


def pack_weight(w, fmt):
    k, n = w.shape
    w = f64(np.asarray(w, np.float32).astype(ml_dtypes.bfloat16)).reshape(k // 32, 32, n)
    amax = np.abs(w).max(1)
    if fmt == "e4m3":
        byte = np.frexp(amax)[1] - 1 + 127 - 7
    else:
        mant, ex = np.frexp(amax / 6.0)
        byte = np.where(mant > 0.5, ex, ex - 1) + 127
    byte = np.clip(np.where(amax > 0, byte, 1), 1, 254)
    scaled = (w * np.exp2(127.0 - byte)[:, None, :]).reshape(k, n).astype(np.float32)
    by_word = np.ascontiguousarray(scaled.reshape(k // 512, 128, 4, n).transpose(0, 1, 3, 2))
    if fmt == "e4m3":
        words = by_word.astype(ml_dtypes.float8_e4m3fn).view(np.uint8)
    else:
        c = by_word.astype(ml_dtypes.float4_e2m1fn).view(np.uint8) & 0xF
        words = (c[..., 0::2] | (c[..., 1::2] << 4)).reshape(k // 512, 128, 2 * n)
    return np.ascontiguousarray(words), np.ascontiguousarray(byte.astype(np.uint8).reshape(k // 512, 16, n))


def unpack_weight(words, scales, fmt):
    g, _, n = scales.shape
    words = np.ascontiguousarray(words).reshape(g, 128, n, -1)
    if fmt == "e4m3":
        vals = words.view(ml_dtypes.float8_e4m3fn).astype(np.float64)
    else:
        nib = np.empty((g, 128, n, 4), np.uint8)
        nib[..., 0::2] = words & 0xF
        nib[..., 1::2] = words >> 4
        vals = E2M1[nib]
    vals = vals * np.repeat(np.exp2(scales.astype(np.float64) - 127.0), 8, axis=1)[..., None]
    return vals.transpose(0, 1, 3, 2).reshape(g * 512, n)


def gelu(v):
    return 0.5 * v * (1.0 + np.tanh(np.sqrt(2.0 / np.pi) * (v + 0.044715 * v**3)))


K, T, S, P, H, N = 1024, 2048, 1024, 512, 1024, 512


def setup_inputs():
    n = np.random.standard_normal
    sk = mx_kscale(K)[:, None]
    u = mx_kscale(H)[:, None]
    tab_words, tab_scales = pack_weight(n((K, T)) * sk, "e4m3")
    w1_words, w1_scales = pack_weight(1.5 * n((K, H)) / np.sqrt(K) / sk, "e2m1")
    w2 = 0.56 * n((K, H)) / np.sqrt(K) / sk
    w3 = n((H, N)) / np.sqrt(H) / u
    gain = np.random.choice([-1.0, 1.0], H) * np.random.uniform(0.5, 2.0, H) * u[:, 0]
    return {
        "tab_words": tab_words, "tab_scales": tab_scales,
        "offs": striped(np.random.permutation(T)[:S]),
        "pos1": striped(np.random.permutation(S)[:P]),
        "pos2": striped(np.random.permutation(S)[:P]),
        "w1_words": w1_words, "w1_scales": w1_scales,
        "w2": w2.astype(np.float32),
        "temp1": np.random.uniform(0.4, 1.6, H).astype(np.float32),
        "shift1": (0.5 * n(H)).astype(np.float32),
        "temp2": np.random.uniform(0.4, 1.6, H).astype(np.float32),
        "lift": np.random.uniform(4.0, 12.0, H).astype(np.float32),
        "gain": gain.astype(np.float32),
        "w3": w3.astype(np.float32),
    }


def reference(tab_words, tab_scales, offs, pos1, pos2, w1_words, w1_scales,
              w2, temp1, shift1, temp2, lift, gain, w3):
    v = unpack_weight(tab_words, tab_scales, "e4m3")[:, unstriped(offs)]
    w1 = unpack_weight(w1_words, w1_scales, "e2m1")
    x1 = w1.T @ v
    x2 = mxq(f64(w2), 0, "e4m3").T @ v
    h = x1 * np.sin(x2)
    a = np.exp(f64(temp1)[:, None] * h[:, unstriped(pos1)] + f64(shift1)[:, None])
    top = h.max(axis=1)
    c = np.exp(f64(temp2)[:, None] * (h[:, unstriped(pos2)] - top[:, None]))
    y = np.sqrt(a + f64(lift)[:, None] * c) * f64(gain)[:, None]
    return mxq(f64(w3), 0, "e4m3").T @ mxq(y, 0, "e4m3")

@@ -1,0 +1,314 @@
+import math
+from contextlib import ExitStack
+
+import concourse.mybir as mybir
+from concourse.masks import make_identity
+
+K, T, S, M, H, N = 1024, 2048, 1024, 512, 1024, 512
+FLOPS = 2 * (2 * K * H * S + H * N * M)
+
+F32 = mybir.dt.float32
+BF16 = mybir.dt.bfloat16
+I32 = mybir.dt.int32
+U32 = mybir.dt.uint32
+U16 = mybir.dt.uint16
+U8 = mybir.dt.uint8
+FP8X4 = mybir.dt.float8_e4m3fn_x4
+FP4X4 = mybir.dt.float4_e2m1fn_x4
+ACT = mybir.ActivationFunctionType
+ALU = mybir.AluOpType
+
+P = 128
+PASSES = 2
+SLOTS = 4
+BANK = 512
+SQUARES_ON_SCALAR = 4
+M_PIECES = ((0, 256), (256, 512))
+TEMP1, SHIFT1, TEMP2, LIFT, GAIN = range(5)
+
+
+def tile_list_electrolyte_recipe_picker_kernel(
+    tc, tab_words, tab_scales, offs, pos1, pos2, w1_words, w1_scales,
+    w2, temp1, shift1, temp2, lift, gain, w3, out
+):
+    nc = tc.nc
+    with ExitStack() as ctx:
+        lists = ctx.enter_context(tc.tile_pool(name="lists", bufs=1))
+        sb = ctx.enter_context(tc.tile_pool(name="sb", bufs=1))
+        ps = ctx.enter_context(tc.psum_pool(name="ps", bufs=1))
+        used = {"x2": [], "x1": []}
+
+        def bank(shape, name, ring):
+            count = len(used[ring])
+            number = count if ring == "x2" and count < 8 else {"x2": 0, "x1": 4}[ring] + count % 4
+            used[ring].append(number)
+            return ps.tile(shape, F32, name=name, tag="bank_%d" % number)
+
+        def tile(shape, dtype, name, tag=None):
+            return sb.tile(shape, dtype, name=name, tag=tag or name, align_bytes=64)
+
+        offs_sb = lists.tile([P, S // 16], U16, name="offs_sb")
+        nc.sync.dma_start(offs_sb[:], offs)
+        pos1_sb = lists.tile([P, M // 16], U16, name="pos1_sb")
+        nc.sync.dma_start(pos1_sb[:], pos1)
+        pos2_sb = lists.tile([P, M // 16], U16, name="pos2_sb")
+        nc.sync.dma_start(pos2_sb[:], pos2)
+
+        def load_w2(a, b):
+            raw = tile([P, SLOTS, BANK], F32, "w2_raw_%d%d" % (a, b), tag="w2_raw_%d" % a)
+            nc.sync.dma_start(
+                out=raw[:],
+                in_=w2[512 * a : 512 * (a + 1), 512 * b : 512 * (b + 1)].rearrange("(p j) c -> p j c", j=SLOTS),
+            )
+            return raw
+
+        w2_raw = {(0, 0): load_w2(0, 0)}
+        tab_scales_sb = tile([P, T], U8, "tab_scales_sb")
+        nc.gpsimd.memset(tab_scales_sb[:].bitcast(I32), 0)
+        for quad in range(4):
+            nc.sync.dma_start(
+                out=tab_scales_sb[32 * quad : 32 * quad + 8, :].bitcast(I32),
+                in_=tab_scales[:, 4 * quad : 4 * quad + 4, :].bitcast(I32),
+            )
+        w2_raw[1, 0] = load_w2(1, 0)
+        ones = tile([P, 1], F32, "ones", tag="tab_words")
+        nc.gpsimd.memset(ones[:], 1.0)
+        quarter_pi = tile([P, 1], F32, "quarter_pi")
+        nc.vector.tensor_scalar(quarter_pi[:], ones[:], math.pi / 4, None, ALU.mult)
+        tab_words_sb = tile([P, PASSES * T], I32, "tab_words_sb", tag="tab_words")
+        for a in range(PASSES):
+            nc.sync.dma_start(
+                out=tab_words_sb[:, T * a : T * (a + 1)], in_=tab_words[a].rearrange("p t i -> p (t i)").bitcast(I32)
+            )
+
+        w1_scales_raw = tile([P, PASSES, H], U8, "w1_scales_raw")
+        nc.vector.memset(w1_scales_raw[:].bitcast(I32), 0)
+        for quad in range(4):
+            nc.gpsimd.dma_start(
+                out=w1_scales_raw[32 * quad : 32 * quad + 4, :, :].bitcast(I32),
+                in_=w1_scales[:, 4 * quad : 4 * quad + 4, :].rearrange("a r e -> r a e").bitcast(I32),
+            )
+
+        identity = tile([P, P], F32, "identity")
+        make_identity(nc, identity[:])
+        v_scales_pass1 = tile([P, S], U8, "v_scales_pass1")
+        nc.vector.memset(v_scales_pass1[:].bitcast(I32), 0)
+
+        v_scales = tile([P, S], U8, "v_scales")
+        nc.vector.tensor_copy(v_scales[:], tab_scales_sb[:].indirect(offs_sb[:]))
+        for quad in range(4):
+            nc.sync.dma_start(
+                out=v_scales_pass1[32 * quad : 32 * quad + 4, :].bitcast(I32),
+                in_=v_scales[32 * quad + 4 : 32 * quad + 8, :].bitcast(I32),
+            )
+        w1_raw = tile([P, PASSES, 2 * H], U8, "w1_raw", tag="tab_scales_sb")
+        nc.sync.dma_start(out=w1_raw[:].bitcast(I32), in_=w1_words.rearrange("a p e -> p a e").bitcast(I32))
+
+        w2_codes = [tile([P, PASSES, BANK], U32, "w2_codes_%d" % b, tag="codes_z_%d" % b) for b in range(PASSES)]
+        w2_scales = [tile([P, PASSES, BANK], U8, "w2_scales_%d" % b, tag="scales_c_%d" % b) for b in range(PASSES)]
+
+        def round_w2(a, b, slots_on_scalar=0):
+            rounded = tile([P, SLOTS, BANK], BF16, "w2_bf16_%d%d" % (a, b), tag="w2_bf16_%d%d" % (a, b))
+            for i in range(SLOTS):
+                copy = nc.scalar.copy if i < slots_on_scalar else nc.vector.tensor_copy
+                copy(
+                    out=rounded[:, i, :].rearrange("p (q g e j) -> p q g j e", g=2, e=4, j=SLOTS),
+                    in_=w2_raw[a, b][:].rearrange("p j (q i g e) -> p i q g j e", i=SLOTS, g=2, e=4)[:, i],
+                )
+            return rounded
+
+        def quantise_w2(a, b, rounded, slots_at_once):
+            for i in range(0, SLOTS, slots_at_once):
+                cols = slice(P * i, P * (i + slots_at_once))
+                nc.vector.quantize_mx(
+                    out=w2_codes[b][:, a, cols].bitcast(FP8X4),
+                    scales=w2_scales[b][:, a, cols],
+                    in_=rounded[:, i : i + slots_at_once, :].rearrange("p i c -> p (i c)"),
+                )
+
+        for a in range(PASSES):
+            quantise_w2(a, 0, round_w2(a, 0, SLOTS * a), SLOTS)
+        for a in range(PASSES):
+            w2_raw[a, 1] = load_w2(a, 1)
+        v_words = []
+        for a in range(PASSES):
+            picked = tile([P, S], U32, "v_words_%d" % a)
+            for half in range(2):
+                nc.vector.tensor_copy(
+                    picked[:, BANK * half : BANK * (half + 1)],
+                    tab_words_sb[:, T * a : T * (a + 1)].bitcast(U32).indirect(offs_sb[:, 32 * half : 32 * (half + 1)]),
+                )
+            v_words.append(picked)
+
+        w1_codes = tile([P, PASSES, 2 * H], U8, "w1_codes", tag="tab_words")
+        nc.vector.tensor_copy(
+            out=w1_codes[:].bitcast(I32).rearrange("p a (b i q w) -> p (a b) i q w", b=2, i=SLOTS, w=4),
+            in_=w1_raw[:].bitcast(I32).rearrange("p a (b q i w) -> p (a b) i q w", b=2, i=SLOTS, w=4),
+        )
+        w1_planes = tile([P, PASSES, H], U8, "w1_planes", tag="w2_bf16_10")
+        nc.vector.tensor_copy(
+            out=w1_planes[:].bitcast(I32).rearrange("p a (b i q w) -> p (a b) i q w", b=2, i=SLOTS, w=2),
+            in_=w1_scales_raw[:].bitcast(I32).rearrange("p a (b q i w) -> p (a b) i q w", b=2, i=SLOTS, w=2),
+        )
+
+        rows = tile([P, PASSES * 20], F32, "rows")
+
+        def row_value(v, b, i):
+            col = 20 * b + 4 * v + i
+            return rows[:, col : col + 1]
+
+        tiles = [(b, i) for b in range(PASSES) for i in range(SLOTS)]
+        h = [tile([P, S], F32, "h_%d" % s) for s in range(len(tiles))]
+        bias2 = tile([P, len(tiles)], F32, "bias2")
+        top = tile([P, len(tiles)], F32, "top")
+
+        def sine_stage(s):
+            b, i = tiles[s]
+            for half in range(2):
+                cols = slice(BANK * half, BANK * (half + 1))
+                x2 = bank([P, BANK], "x2", "x2")
+                for a in range(PASSES):
+                    nc.tensor.matmul_mx(
+                        out=x2[:],
+                        lhsT=w2_codes[b][:, a, P * i : P * (i + 1)].bitcast(FP8X4),
+                        lhsT_scale=w2_scales[b][:, a, P * i : P * (i + 1)],
+                        rhs=v_words[a][:, cols].bitcast(FP8X4),
+                        rhs_scale=v_scales[4 * a : P, cols],
+                        start=(a == 0),
+                        stop=(a == PASSES - 1),
+                    )
+                nc.scalar.activation(h[s][:, cols], x2[:], ACT.Sin, bias=quarter_pi[:], scale=0.5)
+            if s < SQUARES_ON_SCALAR:
+                nc.scalar.activation(h[s][:], h[s][:], ACT.Square)
+            else:
+                nc.vector.tensor_tensor(h[s][:], h[s][:], h[s][:], ALU.mult)
+
+        def product_stage(s):
+            b, i = tiles[s]
+            for half in range(2):
+                cols = slice(BANK * half, BANK * (half + 1))
+                x1 = bank([P, BANK], "x1", "x1")
+                for a in range(PASSES):
+                    nc.tensor.matmul_mx(
+                        out=x1[:],
+                        lhsT=w1_codes[:, a, 2 * P * s : 2 * P * (s + 1)].bitcast(FP4X4),
+                        lhsT_scale=w1_planes[:, a, P * s : P * (s + 1)],
+                        rhs=v_words[a][:, cols].bitcast(FP8X4),
+                        rhs_scale=(v_scales, v_scales_pass1)[a][:, cols],
+                        start=(a == 0),
+                        stop=(a == PASSES - 1),
+                    )
+                nc.vector.scalar_tensor_tensor(h[s][:, cols], h[s][:, cols], 0.5, x1[:], ALU.subtract, ALU.mult)
+            nc.vector.tensor_scalar(h[s][:], h[s][:], 2.0, None, ALU.mult, ALU.max, accum_out=top[:, s : s + 1])
+            first = s if b else 0
+            if b or i == SLOTS - 1:
+                col = 20 * b + 4 * TEMP2
+                nc.vector.scalar_tensor_tensor(
+                    bias2[:, first : s + 1], top[:, first : s + 1], -1.0,
+                    rows[:, col + first % SLOTS : col + i + 1], ALU.mult, ALU.mult,
+                )
+
+        rows_in = tile([P, 2 * P], F32, "rows_in", tag="w2_bf16_00")
+        nc.gpsimd.memset(rows_in[:], 0.0)
+        for v, vec in enumerate((temp1, shift1, temp2, lift, gain)):
+            nc.sync.dma_start(
+                out=rows_in[4 * v : 4 * v + 4, :].rearrange("i (c u) -> i c u", u=8),
+                in_=vec.rearrange("(c i u) -> i c u", i=SLOTS, u=8),
+            )
+        for s in range(SLOTS):
+            sine_stage(s)
+        rows_ps = bank([P, PASSES, P], "rows_ps", "x2")
+        for b in range(PASSES):
+            nc.tensor.transpose(rows_ps[:, b, :], rows_in[:, P * b : P * (b + 1)], identity[:])
+        nc.scalar.copy(rows[:].rearrange("p (b c) -> p b c", b=PASSES), rows_ps[:, :, 0:20])
+        for a in range(PASSES):
+            quantise_w2(a, 1, round_w2(a, 1), SLOTS)
+        for s in range(SLOTS, len(tiles)):
+            product_stage(s - SLOTS)
+            sine_stage(s)
+        w3_raw = [tile([P, SLOTS * N], F32, "w3_raw_%d" % b, tag="w2_raw_%d" % b) for b in range(PASSES)]
+        for b in range(PASSES):
+            for i in range(SLOTS):
+                nc.sync.dma_start(
+                    out=w3_raw[b][:, N * i : N * (i + 1)],
+                    in_=w3[512 * b : 512 * (b + 1), :].rearrange("(q i u) n -> i q u n", i=SLOTS, u=8)[i],
+                )
+
+        z = [tile([P, SLOTS, M], F32, "z_%d" % b, tag="codes_z_%d" % (1 - b)) for b in range(PASSES)]
+        c = [tile([P, SLOTS, M], F32, "c_%d" % b, tag="scales_c_%d" % (1 - b)) for b in range(PASSES)]
+
+        def look_stage(s):
+            b, i = tiles[s]
+            nc.scalar.activation(
+                z[b][:, i, :], h[s][:].indirect(pos1_sb[:]), ACT.Exp,
+                bias=row_value(SHIFT1, b, i), scale=row_value(TEMP1, b, i),
+            )
+            nc.scalar.activation(
+                c[b][:, i, :], h[s][:].indirect(pos2_sb[:]), ACT.Exp,
+                bias=bias2[:, s : s + 1], scale=row_value(TEMP2, b, i),
+            )
+            nc.vector.scalar_tensor_tensor(
+                z[b][:, i, :], c[b][:, i, :], row_value(LIFT, b, i), z[b][:, i, :], ALU.mult, ALU.add
+            )
+
+        w3_codes = tile([P, PASSES, N], U32, "w3_codes")
+        w3_scales = tile([P, PASSES, N], U8, "w3_scales")
+
+        def quantise_w3(b):
+            rounded = tile([P, N * SLOTS], BF16, "w3_bf16_%d" % b, tag="w2_bf16_%d1" % b)
+            nc.vector.tensor_copy(
+                out=rounded[:].rearrange("p (g e i) -> p g i e", e=4, i=SLOTS),
+                in_=w3_raw[b][:].rearrange("p (i g e) -> p g i e", i=SLOTS, e=4),
+            )
+            nc.vector.quantize_mx(out=w3_codes[:, b, :].bitcast(FP8X4), scales=w3_scales[:, b, :], in_=rounded[:])
+
+        for s in range(SLOTS):
+            product_stage(SLOTS + s)
+            look_stage(s)
+        for s in range(SLOTS, len(tiles)):
+            look_stage(s)
+        for b in range(PASSES):
+            quantise_w3(b)
+
+        roots_first = tile([P, SLOTS * M], F32, "roots_0", tag="h_7")
+        roots = [roots_first, tile([P, SLOTS * M], F32, "roots_1")]
+        y = tile([P, PASSES, SLOTS * M], BF16, "y")
+        y_codes = tile([P, PASSES, M], U32, "y_codes")
+        y_scales = tile([P, PASSES, M], U8, "y_scales")
+        result = tile([P, N // P, M], F32, "result")
+        for m0, m1 in M_PIECES:
+            width = m1 - m0
+            for b in range(PASSES):
+                root = roots[b][:, SLOTS * m0 : SLOTS * m1].rearrange("p (m i) -> p m i", i=SLOTS)
+                nc.scalar.activation(root, z[b][:, :, m0:m1].rearrange("p i m -> p m i"), ACT.Sqrt)
+                gains = rows[:, 20 * b + 4 * GAIN : 20 * b + 4 * GAIN + SLOTS]
+                nc.vector.tensor_tensor(
+                    y[:, b, SLOTS * m0 : SLOTS * m1].rearrange("p (m i) -> p m i", i=SLOTS),
+                    root,
+                    gains.unsqueeze(1).to_broadcast([P, width, SLOTS]),
+                    ALU.mult,
+                )
+                nc.vector.quantize_mx(
+                    out=y_codes[:, b, m0:m1].bitcast(FP8X4),
+                    scales=y_scales[:, b, m0:m1],
+                    in_=y[:, b, SLOTS * m0 : SLOTS * m1],
+                )
+            for n in range(N // P):
+                acc = bank([P, width], "acc", ("x2", "x1")[n % 2])
+                for b in range(PASSES):
+                    nc.tensor.matmul_mx(
+                        out=acc[:],
+                        lhsT=w3_codes[:, b, P * n : P * (n + 1)].bitcast(FP8X4),
+                        lhsT_scale=w3_scales[:, b, P * n : P * (n + 1)],
+                        rhs=y_codes[:, b, m0:m1].bitcast(FP8X4),
+                        rhs_scale=y_scales[:, b, m0:m1],
+                        start=(b == 0),
+                        stop=(b == PASSES - 1),
+                    )
+                if n % 2 == 0:
+                    nc.vector.tensor_copy(result[:, n, m0:m1], acc[:])
+                else:
+                    nc.scalar.copy(result[:, n, m0:m1], acc[:])
+            nc.sync.dma_start(
+                out=out[:, m0:m1].rearrange("(n p) m -> p n m", p=P), in_=result[:, :, m0:m1]
+            )

@@ -22,8 +22,8 @@ P = 128
 PASSES = 2
 SLOTS = 4
 BANK = 512
-SQUARES_ON_SCALAR = 4
-M_PIECES = ((0, 256), (256, 512))
+SQUARES_ON_SCALAR = 2
+M_PIECES = ((0, 128), (128, 256), (256, 384), (384, 512))
 TEMP1, SHIFT1, TEMP2, LIFT, GAIN = range(5)
 
 
@@ -39,8 +39,7 @@ def tile_list_electrolyte_recipe_picker_kernel(
         used = {"x2": [], "x1": []}
 
         def bank(shape, name, ring):
-            count = len(used[ring])
-            number = count if ring == "x2" and count < 8 else {"x2": 0, "x1": 4}[ring] + count % 4
+            number = {"x2": 0, "x1": 4}[ring] + len(used[ring]) % 4
             used[ring].append(number)
             return ps.tile(shape, F32, name=name, tag="bank_%d" % number)
 
@@ -54,46 +53,64 @@ def tile_list_electrolyte_recipe_picker_kernel(
         pos2_sb = lists.tile([P, M // 16], U16, name="pos2_sb")
         nc.sync.dma_start(pos2_sb[:], pos2)
 
-        def load_w2(a, b):
-            raw = tile([P, SLOTS, BANK], F32, "w2_raw_%d%d" % (a, b), tag="w2_raw_%d" % a)
-            nc.sync.dma_start(
-                out=raw[:],
-                in_=w2[512 * a : 512 * (a + 1), 512 * b : 512 * (b + 1)].rearrange("(p j) c -> p j c", j=SLOTS),
-            )
-            return raw
-
-        w2_raw = {(0, 0): load_w2(0, 0)}
-        tab_scales_sb = tile([P, T], U8, "tab_scales_sb")
+        tab_words_sb = []
+        for a in range(PASSES):
+            words = tile([P, T], I32, "tab_words_%d" % a, tag="wide_%d" % a)
+            nc.sync.dma_start(out=words[:], in_=tab_words[a].rearrange("p t i -> p (t i)").bitcast(I32))
+            tab_words_sb.append(words)
+        tab_scales_sb = tile([P, T], U8, "tab_scales_sb", tag="wide_2")
         nc.gpsimd.memset(tab_scales_sb[:].bitcast(I32), 0)
         for quad in range(4):
             nc.sync.dma_start(
                 out=tab_scales_sb[32 * quad : 32 * quad + 8, :].bitcast(I32),
                 in_=tab_scales[:, 4 * quad : 4 * quad + 4, :].bitcast(I32),
             )
-        w2_raw[1, 0] = load_w2(1, 0)
-        ones = tile([P, 1], F32, "ones", tag="tab_words")
+        ones = tile([P, 1], F32, "ones", tag="w_raw")
         nc.gpsimd.memset(ones[:], 1.0)
         quarter_pi = tile([P, 1], F32, "quarter_pi")
         nc.vector.tensor_scalar(quarter_pi[:], ones[:], math.pi / 4, None, ALU.mult)
-        tab_words_sb = tile([P, PASSES * T], I32, "tab_words_sb", tag="tab_words")
-        for a in range(PASSES):
+
+        w2_raw = {}
+
+        def load_w2(a, b, raw):
             nc.sync.dma_start(
-                out=tab_words_sb[:, T * a : T * (a + 1)], in_=tab_words[a].rearrange("p t i -> p (t i)").bitcast(I32)
+                out=raw.rearrange("p (j c) -> p j c", j=SLOTS),
+                in_=w2[512 * a : 512 * (a + 1), 512 * b : 512 * (b + 1)].rearrange("(p j) c -> p j c", j=SLOTS),
             )
+            w2_raw[a, b] = raw
+
+        w2_first = tile([P, PASSES * SLOTS * BANK], F32, "w2_first", tag="w_raw")
+        for a in range(PASSES):
+            load_w2(a, 0, w2_first[:, SLOTS * BANK * a : SLOTS * BANK * (a + 1)])
 
         w1_scales_raw = tile([P, PASSES, H], U8, "w1_scales_raw")
-        nc.vector.memset(w1_scales_raw[:].bitcast(I32), 0)
+        nc.gpsimd.memset(w1_scales_raw[:].bitcast(I32), 0)
         for quad in range(4):
-            nc.gpsimd.dma_start(
+            nc.sync.dma_start(
                 out=w1_scales_raw[32 * quad : 32 * quad + 4, :, :].bitcast(I32),
                 in_=w1_scales[:, 4 * quad : 4 * quad + 4, :].rearrange("a r e -> r a e").bitcast(I32),
             )
-
+        rows_raw = tile([P, 512], F32, "rows_raw")
+        for v, vec in enumerate((temp1, shift1, temp2, lift, gain)):
+            nc.gpsimd.dma_start(
+                out=rows_raw[PASSES * v : PASSES * (v + 1), :], in_=vec.rearrange("(b c) -> b c", b=PASSES)
+            )
+        rows_dealt = tile([P, SLOTS, P], F32, "rows_dealt")
+        nc.vector.memset(rows_dealt[:], 0.0)
+        nc.gpsimd.tensor_copy(
+            out=rows_dealt[0:10].rearrange("v i (q u) -> v i q u", u=8),
+            in_=rows_raw[0:10].rearrange("v (q i u) -> v i q u", i=SLOTS, u=8),
+        )
         identity = tile([P, P], F32, "identity")
         make_identity(nc, identity[:])
         v_scales_pass1 = tile([P, S], U8, "v_scales_pass1")
         nc.vector.memset(v_scales_pass1[:].bitcast(I32), 0)
 
+        v_words = []
+        for a in range(PASSES):
+            picked = tile([P, S], U32, "v_words_%d" % a)
+            nc.vector.tensor_copy(picked[:], tab_words_sb[a][:].bitcast(U32).indirect(offs_sb[:]))
+            v_words.append(picked)
         v_scales = tile([P, S], U8, "v_scales")
         nc.vector.tensor_copy(v_scales[:], tab_scales_sb[:].indirect(offs_sb[:]))
         for quad in range(4):
@@ -101,64 +118,64 @@ def tile_list_electrolyte_recipe_picker_kernel(
                 out=v_scales_pass1[32 * quad : 32 * quad + 4, :].bitcast(I32),
                 in_=v_scales[32 * quad + 4 : 32 * quad + 8, :].bitcast(I32),
             )
-        w1_raw = tile([P, PASSES, 2 * H], U8, "w1_raw", tag="tab_scales_sb")
+        w1_raw = tile([P, PASSES, 2 * H], U8, "w1_raw", tag="wide_0")
         nc.sync.dma_start(out=w1_raw[:].bitcast(I32), in_=w1_words.rearrange("a p e -> p a e").bitcast(I32))
+        for a in range(PASSES):
+            load_w2(a, 1, tile([P, SLOTS * BANK], F32, "w2_second_%d" % a, tag="wide_%d" % (a + 1))[:])
 
-        w2_codes = [tile([P, PASSES, BANK], U32, "w2_codes_%d" % b, tag="codes_z_%d" % b) for b in range(PASSES)]
+        w2_codes = [tile([P, PASSES, BANK], U32, "w2_codes_%d" % b, tag="codes_a_%d" % b) for b in range(PASSES)]
         w2_scales = [tile([P, PASSES, BANK], U8, "w2_scales_%d" % b, tag="scales_c_%d" % b) for b in range(PASSES)]
 
-        def round_w2(a, b, slots_on_scalar=0):
-            rounded = tile([P, SLOTS, BANK], BF16, "w2_bf16_%d%d" % (a, b), tag="w2_bf16_%d%d" % (a, b))
+        def quantise_w2(a, b, slots_on_scalar, slots_at_once):
+            rounded = tile([P, SLOTS, BANK], BF16, "w2_bf16_%d%d" % (a, b))
             for i in range(SLOTS):
-                copy = nc.scalar.copy if i < slots_on_scalar else nc.vector.tensor_copy
+                copy = nc.scalar.copy if i in slots_on_scalar else nc.vector.tensor_copy
                 copy(
                     out=rounded[:, i, :].rearrange("p (q g e j) -> p q g j e", g=2, e=4, j=SLOTS),
-                    in_=w2_raw[a, b][:].rearrange("p j (q i g e) -> p i q g j e", i=SLOTS, g=2, e=4)[:, i],
+                    in_=w2_raw[a, b].rearrange("p (j q i g e) -> p i q g j e", j=SLOTS, i=SLOTS, g=2, e=4)[:, i],
                 )
-            return rounded
+                if (i + 1) % slots_at_once == 0:
+                    first = i + 1 - slots_at_once
+                    cols = slice(P * first, P * (i + 1))
+                    nc.vector.quantize_mx(
+                        out=w2_codes[b][:, a, cols].bitcast(FP8X4),
+                        scales=w2_scales[b][:, a, cols],
+                        in_=rounded[:, first : i + 1, :].rearrange("p i c -> p (i c)"),
+                    )
 
-        def quantise_w2(a, b, rounded, slots_at_once):
-            for i in range(0, SLOTS, slots_at_once):
-                cols = slice(P * i, P * (i + slots_at_once))
-                nc.vector.quantize_mx(
-                    out=w2_codes[b][:, a, cols].bitcast(FP8X4),
-                    scales=w2_scales[b][:, a, cols],
-                    in_=rounded[:, i : i + slots_at_once, :].rearrange("p i c -> p (i c)"),
-                )
+        quantise_w2(0, 0, (0, 1, 2), SLOTS)
+        quantise_w2(1, 0, (), 1)
+        quantise_w2(0, 1, (), SLOTS)
+        quantise_w2(1, 1, (), 2)
 
-        for a in range(PASSES):
-            quantise_w2(a, 0, round_w2(a, 0, SLOTS * a), SLOTS)
-        for a in range(PASSES):
-            w2_raw[a, 1] = load_w2(a, 1)
-        v_words = []
-        for a in range(PASSES):
-            picked = tile([P, S], U32, "v_words_%d" % a)
-            for half in range(2):
-                nc.vector.tensor_copy(
-                    picked[:, BANK * half : BANK * (half + 1)],
-                    tab_words_sb[:, T * a : T * (a + 1)].bitcast(U32).indirect(offs_sb[:, 32 * half : 32 * (half + 1)]),
-                )
-            v_words.append(picked)
-
-        w1_codes = tile([P, PASSES, 2 * H], U8, "w1_codes", tag="tab_words")
+        w1_codes = tile([P, PASSES, 2 * H], U8, "w1_codes", tag="w2_bf16_10")
         nc.vector.tensor_copy(
             out=w1_codes[:].bitcast(I32).rearrange("p a (b i q w) -> p (a b) i q w", b=2, i=SLOTS, w=4),
             in_=w1_raw[:].bitcast(I32).rearrange("p a (b q i w) -> p (a b) i q w", b=2, i=SLOTS, w=4),
         )
-        w1_planes = tile([P, PASSES, H], U8, "w1_planes", tag="w2_bf16_10")
+        w1_planes = tile([P, PASSES, H], U8, "w1_planes", tag="w2_bf16_00")
         nc.vector.tensor_copy(
             out=w1_planes[:].bitcast(I32).rearrange("p a (b i q w) -> p (a b) i q w", b=2, i=SLOTS, w=2),
             in_=w1_scales_raw[:].bitcast(I32).rearrange("p a (b q i w) -> p (a b) i q w", b=2, i=SLOTS, w=2),
         )
 
-        rows = tile([P, PASSES * 20], F32, "rows")
+        rows = tile([P, 5 * PASSES * SLOTS], F32, "rows")
 
-        def row_value(v, b, i):
-            col = 20 * b + 4 * v + i
-            return rows[:, col : col + 1]
+        def row_values(v, b, first, count=1):
+            col = SLOTS * (PASSES * v + b) + first
+            return rows[:, col : col + count]
+
+        w3_raw = tile([P, PASSES * SLOTS * N], F32, "w3_raw", tag="w_raw")
+        for b in range(PASSES):
+            for i in range(SLOTS):
+                nc.sync.dma_start(
+                    out=w3_raw[:, N * (SLOTS * b + i) : N * (SLOTS * b + i + 1)],
+                    in_=w3[512 * b : 512 * (b + 1), :].rearrange("(q i u) n -> i q u n", i=SLOTS, u=8)[i],
+                )
 
         tiles = [(b, i) for b in range(PASSES) for i in range(SLOTS)]
         h = [tile([P, S], F32, "h_%d" % s) for s in range(len(tiles))]
+        squares = tile([P, 4 * S], F32, "squares", tag="wide_2")
         bias2 = tile([P, len(tiles)], F32, "bias2")
         top = tile([P, len(tiles)], F32, "top")
 
@@ -180,11 +197,13 @@ def tile_list_electrolyte_recipe_picker_kernel(
                 nc.scalar.activation(h[s][:, cols], x2[:], ACT.Sin, bias=quarter_pi[:], scale=0.5)
             if s < SQUARES_ON_SCALAR:
                 nc.scalar.activation(h[s][:], h[s][:], ACT.Square)
-            else:
-                nc.vector.tensor_tensor(h[s][:], h[s][:], h[s][:], ALU.mult)
 
         def product_stage(s):
             b, i = tiles[s]
+            squared = h[s][:]
+            if s >= SQUARES_ON_SCALAR:
+                squared = squares[:, S * (s % 4) : S * (s % 4 + 1)]
+                nc.gpsimd.tensor_tensor(squared, h[s][:], h[s][:], ALU.mult)
             for half in range(2):
                 cols = slice(BANK * half, BANK * (half + 1))
                 x1 = bank([P, BANK], "x1", "x1")
@@ -198,117 +217,103 @@ def tile_list_electrolyte_recipe_picker_kernel(
                         start=(a == 0),
                         stop=(a == PASSES - 1),
                     )
-                nc.vector.scalar_tensor_tensor(h[s][:, cols], h[s][:, cols], 0.5, x1[:], ALU.subtract, ALU.mult)
+                nc.vector.scalar_tensor_tensor(h[s][:, cols], squared[:, cols], 0.5, x1[:], ALU.subtract, ALU.mult)
             nc.vector.tensor_scalar(h[s][:], h[s][:], 2.0, None, ALU.mult, ALU.max, accum_out=top[:, s : s + 1])
-            first = s if b else 0
-            if b or i == SLOTS - 1:
-                col = 20 * b + 4 * TEMP2
-                nc.vector.scalar_tensor_tensor(
-                    bias2[:, first : s + 1], top[:, first : s + 1], -1.0,
-                    rows[:, col + first % SLOTS : col + i + 1], ALU.mult, ALU.mult,
-                )
-
-        rows_in = tile([P, 2 * P], F32, "rows_in", tag="w2_bf16_00")
-        nc.gpsimd.memset(rows_in[:], 0.0)
-        for v, vec in enumerate((temp1, shift1, temp2, lift, gain)):
-            nc.sync.dma_start(
-                out=rows_in[4 * v : 4 * v + 4, :].rearrange("i (c u) -> i c u", u=8),
-                in_=vec.rearrange("(c i u) -> i c u", i=SLOTS, u=8),
+            nc.vector.tensor_scalar(
+                bias2[:, s : s + 1], top[:, s : s + 1], row_values(TEMP2, b, i), -1.0, ALU.mult, ALU.mult
             )
-        for s in range(SLOTS):
-            sine_stage(s)
-        rows_ps = bank([P, PASSES, P], "rows_ps", "x2")
-        for b in range(PASSES):
-            nc.tensor.transpose(rows_ps[:, b, :], rows_in[:, P * b : P * (b + 1)], identity[:])
-        nc.scalar.copy(rows[:].rearrange("p (b c) -> p b c", b=PASSES), rows_ps[:, :, 0:20])
-        for a in range(PASSES):
-            quantise_w2(a, 1, round_w2(a, 1), SLOTS)
-        for s in range(SLOTS, len(tiles)):
-            product_stage(s - SLOTS)
-            sine_stage(s)
-        w3_raw = [tile([P, SLOTS * N], F32, "w3_raw_%d" % b, tag="w2_raw_%d" % b) for b in range(PASSES)]
-        for b in range(PASSES):
-            for i in range(SLOTS):
-                nc.sync.dma_start(
-                    out=w3_raw[b][:, N * i : N * (i + 1)],
-                    in_=w3[512 * b : 512 * (b + 1), :].rearrange("(q i u) n -> i q u n", i=SLOTS, u=8)[i],
-                )
 
-        z = [tile([P, SLOTS, M], F32, "z_%d" % b, tag="codes_z_%d" % (1 - b)) for b in range(PASSES)]
-        c = [tile([P, SLOTS, M], F32, "c_%d" % b, tag="scales_c_%d" % (1 - b)) for b in range(PASSES)]
+        for s in range(6):
+            sine_stage(s)
+        rows_ps = bank([P, SLOTS, P], "rows_ps", "x2")
+        for i in range(SLOTS):
+            nc.tensor.transpose(rows_ps[:, i, :], rows_dealt[:, i, :], identity[:])
+        nc.scalar.copy(
+            rows[:].rearrange("p (c i) -> p c i", i=SLOTS), rows_ps[:, :, 0:10].rearrange("p i c -> p c i")
+        )
+        for s in range(6, len(tiles)):
+            sine_stage(s)
+        for s in range(len(tiles)):
+            product_stage(s)
 
-        def look_stage(s):
-            b, i = tiles[s]
+        look1 = [tile([P, SLOTS, M], F32, "look1_%d" % b, tag="codes_a_%d" % (1 - b)) for b in range(PASSES)]
+        look2 = [tile([P, SLOTS, M], F32, "look2_%d" % b, tag="scales_c_%d" % (1 - b)) for b in range(PASSES)]
+        z = tile([P, PASSES, SLOTS, M], F32, "z", tag="wide_2")
+        for s, (b, i) in enumerate(tiles):
             nc.scalar.activation(
-                z[b][:, i, :], h[s][:].indirect(pos1_sb[:]), ACT.Exp,
-                bias=row_value(SHIFT1, b, i), scale=row_value(TEMP1, b, i),
+                look1[b][:, i, :], h[s][:].indirect(pos1_sb[:]), ACT.Exp,
+                bias=row_values(SHIFT1, b, i), scale=row_values(TEMP1, b, i),
             )
             nc.scalar.activation(
-                c[b][:, i, :], h[s][:].indirect(pos2_sb[:]), ACT.Exp,
-                bias=bias2[:, s : s + 1], scale=row_value(TEMP2, b, i),
+                look2[b][:, i, :], h[s][:].indirect(pos2_sb[:]), ACT.Exp,
+                bias=bias2[:, s : s + 1], scale=row_values(TEMP2, b, i),
             )
             nc.vector.scalar_tensor_tensor(
-                z[b][:, i, :], c[b][:, i, :], row_value(LIFT, b, i), z[b][:, i, :], ALU.mult, ALU.add
+                z[:, b, i, :], look2[b][:, i, :], row_values(LIFT, b, i), look1[b][:, i, :], ALU.mult, ALU.add
             )
 
-        w3_codes = tile([P, PASSES, N], U32, "w3_codes")
+        w3_codes = tile([P, PASSES, N], U32, "w3_codes", tag="w2_bf16_10")
         w3_scales = tile([P, PASSES, N], U8, "w3_scales")
-
-        def quantise_w3(b):
+        for b in range(PASSES):
             rounded = tile([P, N * SLOTS], BF16, "w3_bf16_%d" % b, tag="w2_bf16_%d1" % b)
-            nc.vector.tensor_copy(
-                out=rounded[:].rearrange("p (g e i) -> p g i e", e=4, i=SLOTS),
-                in_=w3_raw[b][:].rearrange("p (i g e) -> p g i e", i=SLOTS, e=4),
-            )
+            for n0 in range(0, N, P):
+                nc.gpsimd.tensor_scalar(
+                    rounded[:].rearrange("p (n i) -> p n i", i=SLOTS)[:, n0 : n0 + P, :],
+                    w3_raw[:, SLOTS * N * b : SLOTS * N * (b + 1)].rearrange("p (i n) -> p n i", i=SLOTS)[:, n0 : n0 + P, :],
+                    1.0, 0.0, ALU.mult, ALU.add,
+                )
             nc.vector.quantize_mx(out=w3_codes[:, b, :].bitcast(FP8X4), scales=w3_scales[:, b, :], in_=rounded[:])
 
-        for s in range(SLOTS):
-            product_stage(SLOTS + s)
-            look_stage(s)
-        for s in range(SLOTS, len(tiles)):
-            look_stage(s)
-        for b in range(PASSES):
-            quantise_w3(b)
-
-        roots_first = tile([P, SLOTS * M], F32, "roots_0", tag="h_7")
-        roots = [roots_first, tile([P, SLOTS * M], F32, "roots_1")]
+        roots = tile([P, 2, SLOTS * 128], F32, "roots", tag="h_7")
         y = tile([P, PASSES, SLOTS * M], BF16, "y")
         y_codes = tile([P, PASSES, M], U32, "y_codes")
         y_scales = tile([P, PASSES, M], U8, "y_scales")
-        result = tile([P, N // P, M], F32, "result")
-        for m0, m1 in M_PIECES:
-            width = m1 - m0
-            for b in range(PASSES):
-                root = roots[b][:, SLOTS * m0 : SLOTS * m1].rearrange("p (m i) -> p m i", i=SLOTS)
-                nc.scalar.activation(root, z[b][:, :, m0:m1].rearrange("p i m -> p m i"), ACT.Sqrt)
-                gains = rows[:, 20 * b + 4 * GAIN : 20 * b + 4 * GAIN + SLOTS]
-                nc.vector.tensor_tensor(
-                    y[:, b, SLOTS * m0 : SLOTS * m1].rearrange("p (m i) -> p m i", i=SLOTS),
-                    root,
-                    gains.unsqueeze(1).to_broadcast([P, width, SLOTS]),
-                    ALU.mult,
-                )
-                nc.vector.quantize_mx(
-                    out=y_codes[:, b, m0:m1].bitcast(FP8X4),
-                    scales=y_scales[:, b, m0:m1],
-                    in_=y[:, b, SLOTS * m0 : SLOTS * m1],
-                )
-            for n in range(N // P):
-                acc = bank([P, width], "acc", ("x2", "x1")[n % 2])
-                for b in range(PASSES):
+        result = tile([P, N // P, M], F32, "result", tag="wide_0")
+
+        def make_y(b, m0, m1):
+            root = roots[:, (PASSES * M_PIECES.index((m0, m1)) + b) % 2, 0 : SLOTS * (m1 - m0)].rearrange("p (m i) -> p m i", i=SLOTS)
+            nc.scalar.activation(root, z[:, b, :, m0:m1].rearrange("p i m -> p m i"), ACT.Sqrt)
+            nc.vector.tensor_tensor(
+                y[:, b, SLOTS * m0 : SLOTS * m1].rearrange("p (m i) -> p m i", i=SLOTS),
+                root,
+                row_values(GAIN, b, 0, SLOTS).unsqueeze(1).to_broadcast([P, m1 - m0, SLOTS]),
+                ALU.mult,
+            )
+
+        def quantise_y(b, m0, m1):
+            nc.vector.quantize_mx(
+                out=y_codes[:, b, m0:m1].bitcast(FP8X4),
+                scales=y_scales[:, b, m0:m1],
+                in_=y[:, b, SLOTS * m0 : SLOTS * m1],
+            )
+
+        def last_product(acc, b, m0, m1):
+            for pair in range(2):
+                for k in range(2):
+                    n = 2 * pair + k
                     nc.tensor.matmul_mx(
-                        out=acc[:],
+                        out=acc[pair][:, k, :],
                         lhsT=w3_codes[:, b, P * n : P * (n + 1)].bitcast(FP8X4),
                         lhsT_scale=w3_scales[:, b, P * n : P * (n + 1)],
                         rhs=y_codes[:, b, m0:m1].bitcast(FP8X4),
                         rhs_scale=y_scales[:, b, m0:m1],
-                        start=(b == 0),
-                        stop=(b == PASSES - 1),
+                        start=(b == 0 and k == 0),
+                        stop=(b == PASSES - 1 and k == 1),
                     )
-                if n % 2 == 0:
-                    nc.vector.tensor_copy(result[:, n, m0:m1], acc[:])
-                else:
-                    nc.scalar.copy(result[:, n, m0:m1], acc[:])
-            nc.sync.dma_start(
-                out=out[:, m0:m1].rearrange("(n p) m -> p n m", p=P), in_=result[:, :, m0:m1]
-            )
+
+        sums = {}
+        for m0, m1 in M_PIECES:
+            sums[m0] = [bank([P, 2, m1 - m0], "acc", ring) for ring in ("x2", "x1")]
+            for b in range(PASSES):
+                make_y(b, m0, m1)
+                quantise_y(b, m0, m1)
+                last_product(sums[m0], b, m0, m1)
+        for m0, m1 in M_PIECES:
+            for pair in range(2):
+                rows_out = slice(2 * pair, 2 * pair + 2)
+                copy = nc.vector.tensor_copy if pair == 0 and m1 == M else nc.scalar.copy
+                copy(result[:, rows_out, m0:m1], sums[m0][pair][:])
+                nc.sync.dma_start(
+                    out=out[:, m0:m1].rearrange("(n p) m -> p n m", p=P)[:, rows_out, :],
+                    in_=result[:, rows_out, m0:m1],
+                )

@@ -22,7 +22,7 @@ P = 128
 PASSES = 2
 SLOTS = 4
 BANK = 512
-SQUARES_ON_SCALAR = 2
+SQUARES_ON_SCALAR = 1
 M_PIECES = ((0, 128), (128, 256), (256, 384), (384, 512))
 TEMP1, SHIFT1, TEMP2, LIFT, GAIN = range(5)
 
@@ -39,7 +39,8 @@ def tile_list_electrolyte_recipe_picker_kernel(
         used = {"x2": [], "x1": []}
 
         def bank(shape, name, ring):
-            number = {"x2": 0, "x1": 4}[ring] + len(used[ring]) % 4
+            count = len(used[ring])
+            number = count if ring == "x2" and count < 8 else {"x2": 0, "x1": 4}[ring] + count % 4
             used[ring].append(number)
             return ps.tile(shape, F32, name=name, tag="bank_%d" % number)
 
@@ -83,13 +84,6 @@ def tile_list_electrolyte_recipe_picker_kernel(
         for a in range(PASSES):
             load_w2(a, 0, w2_first[:, SLOTS * BANK * a : SLOTS * BANK * (a + 1)])
 
-        w1_scales_raw = tile([P, PASSES, H], U8, "w1_scales_raw")
-        nc.gpsimd.memset(w1_scales_raw[:].bitcast(I32), 0)
-        for quad in range(4):
-            nc.sync.dma_start(
-                out=w1_scales_raw[32 * quad : 32 * quad + 4, :, :].bitcast(I32),
-                in_=w1_scales[:, 4 * quad : 4 * quad + 4, :].rearrange("a r e -> r a e").bitcast(I32),
-            )
         rows_raw = tile([P, 512], F32, "rows_raw")
         for v, vec in enumerate((temp1, shift1, temp2, lift, gain)):
             nc.gpsimd.dma_start(
@@ -97,10 +91,17 @@ def tile_list_electrolyte_recipe_picker_kernel(
             )
         rows_dealt = tile([P, SLOTS, P], F32, "rows_dealt")
         nc.vector.memset(rows_dealt[:], 0.0)
-        nc.gpsimd.tensor_copy(
+        nc.scalar.copy(
             out=rows_dealt[0:10].rearrange("v i (q u) -> v i q u", u=8),
             in_=rows_raw[0:10].rearrange("v (q i u) -> v i q u", i=SLOTS, u=8),
         )
+        w1_scales_raw = tile([P, PASSES, H], U8, "w1_scales_raw")
+        nc.gpsimd.memset(w1_scales_raw[:].bitcast(I32), 0)
+        for quad in range(4):
+            nc.sync.dma_start(
+                out=w1_scales_raw[32 * quad : 32 * quad + 4, :, :].bitcast(I32),
+                in_=w1_scales[:, 4 * quad : 4 * quad + 4, :].rearrange("a r e -> r a e").bitcast(I32),
+            )
         identity = tile([P, P], F32, "identity")
         make_identity(nc, identity[:])
         v_scales_pass1 = tile([P, S], U8, "v_scales_pass1")
@@ -118,10 +119,10 @@ def tile_list_electrolyte_recipe_picker_kernel(
                 out=v_scales_pass1[32 * quad : 32 * quad + 4, :].bitcast(I32),
                 in_=v_scales[32 * quad + 4 : 32 * quad + 8, :].bitcast(I32),
             )
-        w1_raw = tile([P, PASSES, 2 * H], U8, "w1_raw", tag="wide_0")
+        w1_raw = tile([P, PASSES, 2 * H], U8, "w1_raw", tag="wide_1")
         nc.sync.dma_start(out=w1_raw[:].bitcast(I32), in_=w1_words.rearrange("a p e -> p a e").bitcast(I32))
         for a in range(PASSES):
-            load_w2(a, 1, tile([P, SLOTS * BANK], F32, "w2_second_%d" % a, tag="wide_%d" % (a + 1))[:])
+            load_w2(a, 1, tile([P, SLOTS * BANK], F32, "w2_second_%d" % a, tag="wide_%d" % (2 * a))[:])
 
         w2_codes = [tile([P, PASSES, BANK], U32, "w2_codes_%d" % b, tag="codes_a_%d" % b) for b in range(PASSES)]
         w2_scales = [tile([P, PASSES, BANK], U8, "w2_scales_%d" % b, tag="scales_c_%d" % b) for b in range(PASSES)]
@@ -131,8 +132,8 @@ def tile_list_electrolyte_recipe_picker_kernel(
             for i in range(SLOTS):
                 copy = nc.scalar.copy if i in slots_on_scalar else nc.vector.tensor_copy
                 copy(
-                    out=rounded[:, i, :].rearrange("p (q g e j) -> p q g j e", g=2, e=4, j=SLOTS),
-                    in_=w2_raw[a, b].rearrange("p (j q i g e) -> p i q g j e", j=SLOTS, i=SLOTS, g=2, e=4)[:, i],
+                    out=rounded[:, i, :].rearrange("p (q u j) -> p q u j", u=8, j=SLOTS),
+                    in_=w2_raw[a, b].rearrange("p (j q i u) -> p i q u j", j=SLOTS, i=SLOTS, u=8)[:, i],
                 )
                 if (i + 1) % slots_at_once == 0:
                     first = i + 1 - slots_at_once
@@ -148,12 +149,12 @@ def tile_list_electrolyte_recipe_picker_kernel(
         quantise_w2(0, 1, (), SLOTS)
         quantise_w2(1, 1, (), 2)
 
-        w1_codes = tile([P, PASSES, 2 * H], U8, "w1_codes", tag="w2_bf16_10")
+        w1_codes = tile([P, PASSES, 2 * H], U8, "w1_codes", tag="w2_bf16_01")
         nc.vector.tensor_copy(
             out=w1_codes[:].bitcast(I32).rearrange("p a (b i q w) -> p (a b) i q w", b=2, i=SLOTS, w=4),
             in_=w1_raw[:].bitcast(I32).rearrange("p a (b q i w) -> p (a b) i q w", b=2, i=SLOTS, w=4),
         )
-        w1_planes = tile([P, PASSES, H], U8, "w1_planes", tag="w2_bf16_00")
+        w1_planes = tile([P, PASSES, H], U8, "w1_planes", tag="wide_0")
         nc.vector.tensor_copy(
             out=w1_planes[:].bitcast(I32).rearrange("p a (b i q w) -> p (a b) i q w", b=2, i=SLOTS, w=2),
             in_=w1_scales_raw[:].bitcast(I32).rearrange("p a (b q i w) -> p (a b) i q w", b=2, i=SLOTS, w=2),
@@ -165,7 +166,7 @@ def tile_list_electrolyte_recipe_picker_kernel(
             col = SLOTS * (PASSES * v + b) + first
             return rows[:, col : col + count]
 
-        w3_raw = tile([P, PASSES * SLOTS * N], F32, "w3_raw", tag="w_raw")
+        w3_raw = tile([P, PASSES * SLOTS * N], F32, "w3_raw", tag="w1_scales_raw")
         for b in range(PASSES):
             for i in range(SLOTS):
                 nc.sync.dma_start(
@@ -174,10 +175,14 @@ def tile_list_electrolyte_recipe_picker_kernel(
                 )
 
         tiles = [(b, i) for b in range(PASSES) for i in range(SLOTS)]
-        h = [tile([P, S], F32, "h_%d" % s) for s in range(len(tiles))]
-        squares = tile([P, 4 * S], F32, "squares", tag="wide_2")
+        sines = [tile([P, S], F32, "h_%d" % s) for s in range(len(tiles))]
+        h = [tile([P, S], F32, "h_first", tag="wide_2")] + sines[1:]
+        squares = tile([P, 4 * S], F32, "squares", tag="w2_bf16_11")
         bias2 = tile([P, len(tiles)], F32, "bias2")
         top = tile([P, len(tiles)], F32, "top")
+
+        def square_of(s):
+            return sines[s][:] if s < SQUARES_ON_SCALAR else squares[:, S * (s % 4) : S * (s % 4 + 1)]
 
         def sine_stage(s):
             b, i = tiles[s]
@@ -194,16 +199,15 @@ def tile_list_electrolyte_recipe_picker_kernel(
                         start=(a == 0),
                         stop=(a == PASSES - 1),
                     )
-                nc.scalar.activation(h[s][:, cols], x2[:], ACT.Sin, bias=quarter_pi[:], scale=0.5)
+                nc.scalar.activation(sines[s][:, cols], x2[:], ACT.Sin, bias=quarter_pi[:], scale=0.5)
             if s < SQUARES_ON_SCALAR:
-                nc.scalar.activation(h[s][:], h[s][:], ACT.Square)
+                nc.scalar.activation(square_of(s), sines[s][:], ACT.Square)
 
         def product_stage(s):
             b, i = tiles[s]
-            squared = h[s][:]
+            squared = square_of(s)
             if s >= SQUARES_ON_SCALAR:
-                squared = squares[:, S * (s % 4) : S * (s % 4 + 1)]
-                nc.gpsimd.tensor_tensor(squared, h[s][:], h[s][:], ALU.mult)
+                nc.gpsimd.tensor_tensor(squared, sines[s][:], sines[s][:], ALU.mult)
             for half in range(2):
                 cols = slice(BANK * half, BANK * (half + 1))
                 x1 = bank([P, BANK], "x1", "x1")
@@ -219,27 +223,25 @@ def tile_list_electrolyte_recipe_picker_kernel(
                     )
                 nc.vector.scalar_tensor_tensor(h[s][:, cols], squared[:, cols], 0.5, x1[:], ALU.subtract, ALU.mult)
             nc.vector.tensor_scalar(h[s][:], h[s][:], 2.0, None, ALU.mult, ALU.max, accum_out=top[:, s : s + 1])
-            nc.vector.tensor_scalar(
-                bias2[:, s : s + 1], top[:, s : s + 1], row_values(TEMP2, b, i), -1.0, ALU.mult, ALU.mult
-            )
 
-        for s in range(6):
-            sine_stage(s)
-        rows_ps = bank([P, SLOTS, P], "rows_ps", "x2")
+        rows_ps = ps.tile([P, SLOTS, P], F32, name="rows_ps", tag="bank_7")
         for i in range(SLOTS):
             nc.tensor.transpose(rows_ps[:, i, :], rows_dealt[:, i, :], identity[:])
         nc.scalar.copy(
             rows[:].rearrange("p (c i) -> p c i", i=SLOTS), rows_ps[:, :, 0:10].rearrange("p i c -> p c i")
         )
-        for s in range(6, len(tiles)):
+        minus_temp2 = tile([P, len(tiles)], F32, "minus_temp2")
+        nc.scalar.activation(minus_temp2[:], row_values(TEMP2, 0, 0, len(tiles)), ACT.Copy, scale=-1.0)
+        for s in range(len(tiles)):
             sine_stage(s)
         for s in range(len(tiles)):
             product_stage(s)
 
         look1 = [tile([P, SLOTS, M], F32, "look1_%d" % b, tag="codes_a_%d" % (1 - b)) for b in range(PASSES)]
         look2 = [tile([P, SLOTS, M], F32, "look2_%d" % b, tag="scales_c_%d" % (1 - b)) for b in range(PASSES)]
-        z = tile([P, PASSES, SLOTS, M], F32, "z", tag="wide_2")
+        z = tile([P, PASSES, SLOTS, M], F32, "z", tag="w2_bf16_11")
         for s, (b, i) in enumerate(tiles):
+            nc.scalar.activation(bias2[:, s : s + 1], top[:, s : s + 1], ACT.Copy, scale=minus_temp2[:, s : s + 1])
             nc.scalar.activation(
                 look1[b][:, i, :], h[s][:].indirect(pos1_sb[:]), ACT.Exp,
                 bias=row_values(SHIFT1, b, i), scale=row_values(TEMP1, b, i),
@@ -252,23 +254,24 @@ def tile_list_electrolyte_recipe_picker_kernel(
                 z[:, b, i, :], look2[b][:, i, :], row_values(LIFT, b, i), look1[b][:, i, :], ALU.mult, ALU.add
             )
 
-        w3_codes = tile([P, PASSES, N], U32, "w3_codes", tag="w2_bf16_10")
+        w3_codes = tile([P, PASSES, N], U32, "w3_codes", tag="w2_bf16_01")
         w3_scales = tile([P, PASSES, N], U8, "w3_scales")
+        w3_rounded = tile([P, PASSES * N * SLOTS], BF16, "w3_bf16", tag="w_raw")
         for b in range(PASSES):
-            rounded = tile([P, N * SLOTS], BF16, "w3_bf16_%d" % b, tag="w2_bf16_%d1" % b)
+            rounded = w3_rounded[:, N * SLOTS * b : N * SLOTS * (b + 1)]
             for n0 in range(0, N, P):
                 nc.gpsimd.tensor_scalar(
-                    rounded[:].rearrange("p (n i) -> p n i", i=SLOTS)[:, n0 : n0 + P, :],
+                    rounded.rearrange("p (n i) -> p n i", i=SLOTS)[:, n0 : n0 + P, :],
                     w3_raw[:, SLOTS * N * b : SLOTS * N * (b + 1)].rearrange("p (i n) -> p n i", i=SLOTS)[:, n0 : n0 + P, :],
                     1.0, 0.0, ALU.mult, ALU.add,
                 )
-            nc.vector.quantize_mx(out=w3_codes[:, b, :].bitcast(FP8X4), scales=w3_scales[:, b, :], in_=rounded[:])
+            nc.vector.quantize_mx(out=w3_codes[:, b, :].bitcast(FP8X4), scales=w3_scales[:, b, :], in_=rounded)
 
         roots = tile([P, 2, SLOTS * 128], F32, "roots", tag="h_7")
         y = tile([P, PASSES, SLOTS * M], BF16, "y")
         y_codes = tile([P, PASSES, M], U32, "y_codes")
         y_scales = tile([P, PASSES, M], U8, "y_scales")
-        result = tile([P, N // P, M], F32, "result", tag="wide_0")
+        result = tile([P, N // P, M], F32, "result", tag="wide_1")
 
         def make_y(b, m0, m1):
             root = roots[:, (PASSES * M_PIECES.index((m0, m1)) + b) % 2, 0 : SLOTS * (m1 - m0)].rearrange("p (m i) -> p m i", i=SLOTS)

@@ -19,12 +19,19 @@ ACT = mybir.ActivationFunctionType
 ALU = mybir.AluOpType
 
 P = 128
+PACK = 4
+PASS = P * PACK
 PASSES = 2
-SLOTS = 4
+RUN = 8
+QUADRANTS = 4
 BANK = 512
+BANKS = 8
+LIST_COLUMN = 16
 SQUARES_ON_SCALAR = 1
-M_PIECES = ((0, 128), (128, 256), (256, 384), (384, 512))
+SQUARE_BUFFERS = 4
+M_PIECE = 128
 TEMP1, SHIFT1, TEMP2, LIFT, GAIN = range(5)
+ROW_VECTORS = 5
 
 
 def tile_list_electrolyte_recipe_picker_kernel(
@@ -36,71 +43,69 @@ def tile_list_electrolyte_recipe_picker_kernel(
         lists = ctx.enter_context(tc.tile_pool(name="lists", bufs=1))
         sb = ctx.enter_context(tc.tile_pool(name="sb", bufs=1))
         ps = ctx.enter_context(tc.psum_pool(name="ps", bufs=1))
-        used = {"x2": [], "x1": []}
+
+        taken = {"low": [], "high": []}
 
         def bank(shape, name, ring):
-            count = len(used[ring])
-            number = count if ring == "x2" and count < 8 else {"x2": 0, "x1": 4}[ring] + count % 4
-            used[ring].append(number)
+            count = len(taken[ring])
+            half_of_banks = BANKS // 2
+            first = {"low": 0, "high": half_of_banks}[ring]
+            number = count if ring == "low" and count < BANKS else first + count % half_of_banks
+            taken[ring].append(number)
             return ps.tile(shape, F32, name=name, tag="bank_%d" % number)
 
         def tile(shape, dtype, name, tag=None):
             return sb.tile(shape, dtype, name=name, tag=tag or name, align_bytes=64)
 
-        offs_sb = lists.tile([P, S // 16], U16, name="offs_sb")
+        offs_sb = lists.tile([P, S // LIST_COLUMN], U16, name="offs_sb")
         nc.sync.dma_start(offs_sb[:], offs)
-        pos1_sb = lists.tile([P, M // 16], U16, name="pos1_sb")
+        pos1_sb = lists.tile([P, M // LIST_COLUMN], U16, name="pos1_sb")
         nc.sync.dma_start(pos1_sb[:], pos1)
-        pos2_sb = lists.tile([P, M // 16], U16, name="pos2_sb")
+        pos2_sb = lists.tile([P, M // LIST_COLUMN], U16, name="pos2_sb")
         nc.sync.dma_start(pos2_sb[:], pos2)
 
         tab_words_sb = []
         for a in range(PASSES):
-            words = tile([P, T], I32, "tab_words_%d" % a, tag="wide_%d" % a)
+            words = tile([P, T], I32, "tab_words_%d" % a, tag="stage_%d" % a)
             nc.sync.dma_start(out=words[:], in_=tab_words[a].rearrange("p t i -> p (t i)").bitcast(I32))
             tab_words_sb.append(words)
-        tab_scales_sb = tile([P, T], U8, "tab_scales_sb", tag="wide_2")
+        tab_scales_sb = tile([P, T], U8, "tab_scales_sb", tag="stage_2")
         nc.gpsimd.memset(tab_scales_sb[:].bitcast(I32), 0)
-        for quad in range(4):
+        for quad in range(QUADRANTS):
             nc.sync.dma_start(
                 out=tab_scales_sb[32 * quad : 32 * quad + 8, :].bitcast(I32),
                 in_=tab_scales[:, 4 * quad : 4 * quad + 4, :].bitcast(I32),
             )
-        ones = tile([P, 1], F32, "ones", tag="w_raw")
-        nc.gpsimd.memset(ones[:], 1.0)
+        one = tile([P, 1], F32, "one", tag="stage_3")
+        nc.gpsimd.memset(one[:], 1.0)
         quarter_pi = tile([P, 1], F32, "quarter_pi")
-        nc.vector.tensor_scalar(quarter_pi[:], ones[:], math.pi / 4, None, ALU.mult)
+        nc.vector.tensor_scalar(quarter_pi[:], one[:], math.pi / 4, None, ALU.mult)
 
         w2_raw = {}
 
         def load_w2(a, b, raw):
             nc.sync.dma_start(
-                out=raw.rearrange("p (j c) -> p j c", j=SLOTS),
-                in_=w2[512 * a : 512 * (a + 1), 512 * b : 512 * (b + 1)].rearrange("(p j) c -> p j c", j=SLOTS),
+                out=raw.rearrange("p (j c) -> p j c", j=PACK),
+                in_=w2[PASS * a : PASS * (a + 1), PASS * b : PASS * (b + 1)].rearrange("(p j) c -> p j c", j=PACK),
             )
             w2_raw[a, b] = raw
 
-        w2_first = tile([P, PASSES * SLOTS * BANK], F32, "w2_first", tag="w_raw")
+        w2_first = tile([P, PASSES * PACK * PASS], F32, "w2_first", tag="stage_3")
         for a in range(PASSES):
-            load_w2(a, 0, w2_first[:, SLOTS * BANK * a : SLOTS * BANK * (a + 1)])
+            load_w2(a, 0, w2_first[:, PACK * PASS * a : PACK * PASS * (a + 1)])
 
-        rows_raw = tile([P, 512], F32, "rows_raw")
-        for v, vec in enumerate((temp1, shift1, temp2, lift, gain)):
-            nc.gpsimd.dma_start(
-                out=rows_raw[PASSES * v : PASSES * (v + 1), :], in_=vec.rearrange("(b c) -> b c", b=PASSES)
-            )
-        rows_dealt = tile([P, SLOTS, P], F32, "rows_dealt")
-        nc.vector.memset(rows_dealt[:], 0.0)
-        nc.scalar.copy(
-            out=rows_dealt[0:10].rearrange("v i (q u) -> v i q u", u=8),
-            in_=rows_raw[0:10].rearrange("v (q i u) -> v i q u", i=SLOTS, u=8),
-        )
-        w1_scales_raw = tile([P, PASSES, H], U8, "w1_scales_raw")
+        w1_scales_raw = tile([P, PASSES, H], U8, "w1_scales_raw", tag="stage_4")
         nc.gpsimd.memset(w1_scales_raw[:].bitcast(I32), 0)
-        for quad in range(4):
+        for quad in range(QUADRANTS):
             nc.sync.dma_start(
                 out=w1_scales_raw[32 * quad : 32 * quad + 4, :, :].bitcast(I32),
                 in_=w1_scales[:, 4 * quad : 4 * quad + 4, :].rearrange("a r e -> r a e").bitcast(I32),
+            )
+        rows_raw = tile([P, PASS], F32, "rows_raw")
+        nc.vector.memset(rows_raw[:], 0.0)
+        for v, vec in enumerate((temp1, shift1, temp2, lift, gain)):
+            nc.gpsimd.dma_start(
+                out=rows_raw[PASSES * v : PASSES * (v + 1), :], in_=vec.rearrange("(b c) -> b c", b=PASSES)
             )
         identity = tile([P, P], F32, "identity")
         make_identity(nc, identity[:])
@@ -114,29 +119,29 @@ def tile_list_electrolyte_recipe_picker_kernel(
             v_words.append(picked)
         v_scales = tile([P, S], U8, "v_scales")
         nc.vector.tensor_copy(v_scales[:], tab_scales_sb[:].indirect(offs_sb[:]))
-        for quad in range(4):
+        for quad in range(QUADRANTS):
             nc.sync.dma_start(
                 out=v_scales_pass1[32 * quad : 32 * quad + 4, :].bitcast(I32),
                 in_=v_scales[32 * quad + 4 : 32 * quad + 8, :].bitcast(I32),
             )
-        w1_raw = tile([P, PASSES, 2 * H], U8, "w1_raw", tag="wide_1")
+        w1_raw = tile([P, PASSES, 2 * H], U8, "w1_raw", tag="stage_1")
         nc.sync.dma_start(out=w1_raw[:].bitcast(I32), in_=w1_words.rearrange("a p e -> p a e").bitcast(I32))
-        for a in range(PASSES):
-            load_w2(a, 1, tile([P, SLOTS * BANK], F32, "w2_second_%d" % a, tag="wide_%d" % (2 * a))[:])
+        for a, stage in enumerate(("stage_0", "stage_2")):
+            load_w2(a, 1, tile([P, PACK * PASS], F32, "w2_second_%d" % a, tag=stage)[:])
 
-        w2_codes = [tile([P, PASSES, BANK], U32, "w2_codes_%d" % b, tag="codes_a_%d" % b) for b in range(PASSES)]
-        w2_scales = [tile([P, PASSES, BANK], U8, "w2_scales_%d" % b, tag="scales_c_%d" % b) for b in range(PASSES)]
+        w2_codes = [tile([P, PASSES, PASS], U32, "w2_codes_%d" % b) for b in range(PASSES)]
+        w2_scales = [tile([P, PASSES, PASS], U8, "w2_scales_%d" % b) for b in range(PASSES)]
 
-        def quantise_w2(a, b, slots_on_scalar, slots_at_once):
-            rounded = tile([P, SLOTS, BANK], BF16, "w2_bf16_%d%d" % (a, b))
-            for i in range(SLOTS):
-                copy = nc.scalar.copy if i in slots_on_scalar else nc.vector.tensor_copy
+        def quantise_w2(a, b, tiles_on_scalar, tiles_at_once):
+            rounded = tile([P, PACK, PASS], BF16, "w2_bf16_%d%d" % (a, b))
+            for i in range(PACK):
+                copy = nc.scalar.copy if i < tiles_on_scalar else nc.vector.tensor_copy
                 copy(
-                    out=rounded[:, i, :].rearrange("p (q u j) -> p q u j", u=8, j=SLOTS),
-                    in_=w2_raw[a, b].rearrange("p (j q i u) -> p i q u j", j=SLOTS, i=SLOTS, u=8)[:, i],
+                    out=rounded[:, i, :].rearrange("p (q u j) -> p q u j", u=RUN, j=PACK),
+                    in_=w2_raw[a, b].rearrange("p (j q i u) -> p i q u j", j=PACK, i=PACK, u=RUN)[:, i],
                 )
-                if (i + 1) % slots_at_once == 0:
-                    first = i + 1 - slots_at_once
+                if (i + 1) % tiles_at_once == 0:
+                    first = i + 1 - tiles_at_once
                     cols = slice(P * first, P * (i + 1))
                     nc.vector.quantize_mx(
                         out=w2_codes[b][:, a, cols].bitcast(FP8X4),
@@ -144,51 +149,52 @@ def tile_list_electrolyte_recipe_picker_kernel(
                         in_=rounded[:, first : i + 1, :].rearrange("p i c -> p (i c)"),
                     )
 
-        quantise_w2(0, 0, (0, 1, 2), SLOTS)
-        quantise_w2(1, 0, (), 1)
-        quantise_w2(0, 1, (), SLOTS)
-        quantise_w2(1, 1, (), 2)
+        quantise_w2(0, 0, 3, PACK)
+        quantise_w2(1, 0, 0, 1)
+        quantise_w2(0, 1, 0, PACK)
+        quantise_w2(1, 1, 0, 2)
 
         w1_codes = tile([P, PASSES, 2 * H], U8, "w1_codes", tag="w2_bf16_01")
         nc.vector.tensor_copy(
-            out=w1_codes[:].bitcast(I32).rearrange("p a (b i q w) -> p (a b) i q w", b=2, i=SLOTS, w=4),
-            in_=w1_raw[:].bitcast(I32).rearrange("p a (b q i w) -> p (a b) i q w", b=2, i=SLOTS, w=4),
+            out=w1_codes[:].bitcast(I32).rearrange("p a (b i q w) -> p (a b) i q w", b=PASSES, i=PACK, w=4),
+            in_=w1_raw[:].bitcast(I32).rearrange("p a (b q i w) -> p (a b) i q w", b=PASSES, i=PACK, w=4),
         )
-        w1_planes = tile([P, PASSES, H], U8, "w1_planes", tag="wide_0")
+        w1_planes = tile([P, PASSES, H], U8, "w1_planes", tag="stage_0")
         nc.vector.tensor_copy(
-            out=w1_planes[:].bitcast(I32).rearrange("p a (b i q w) -> p (a b) i q w", b=2, i=SLOTS, w=2),
-            in_=w1_scales_raw[:].bitcast(I32).rearrange("p a (b q i w) -> p (a b) i q w", b=2, i=SLOTS, w=2),
+            out=w1_planes[:].bitcast(I32).rearrange("p a (b i q w) -> p (a b) i q w", b=PASSES, i=PACK, w=2),
+            in_=w1_scales_raw[:].bitcast(I32).rearrange("p a (b q i w) -> p (a b) i q w", b=PASSES, i=PACK, w=2),
         )
 
-        rows = tile([P, 5 * PASSES * SLOTS], F32, "rows")
+        rows = tile([P, ROW_VECTORS * PASSES * PACK], F32, "rows")
 
         def row_values(v, b, first, count=1):
-            col = SLOTS * (PASSES * v + b) + first
+            col = PACK * (PASSES * v + b) + first
             return rows[:, col : col + count]
 
-        w3_raw = tile([P, PASSES * SLOTS * N], F32, "w3_raw", tag="w1_scales_raw")
+        w3_raw = tile([P, PASSES * PACK * N], F32, "w3_raw", tag="stage_4")
         for b in range(PASSES):
-            for i in range(SLOTS):
+            for i in range(PACK):
                 nc.sync.dma_start(
-                    out=w3_raw[:, N * (SLOTS * b + i) : N * (SLOTS * b + i + 1)],
-                    in_=w3[512 * b : 512 * (b + 1), :].rearrange("(q i u) n -> i q u n", i=SLOTS, u=8)[i],
+                    out=w3_raw[:, N * (PACK * b + i) : N * (PACK * b + i + 1)],
+                    in_=w3[PASS * b : PASS * (b + 1), :].rearrange("(q i u) n -> i q u n", i=PACK, u=RUN)[i],
                 )
 
-        tiles = [(b, i) for b in range(PASSES) for i in range(SLOTS)]
-        sines = [tile([P, S], F32, "h_%d" % s) for s in range(len(tiles))]
-        h = [tile([P, S], F32, "h_first", tag="wide_2")] + sines[1:]
-        squares = tile([P, 4 * S], F32, "squares", tag="w2_bf16_11")
-        bias2 = tile([P, len(tiles)], F32, "bias2")
-        top = tile([P, len(tiles)], F32, "top")
+        row_tiles = [(b, i) for b in range(PASSES) for i in range(PACK)]
+        sines = [tile([P, S], F32, "sine_%d" % s) for s in range(len(row_tiles))]
+        h = [tile([P, S], F32, "h_first", tag="stage_2")] + sines[1:]
+        squares = tile([P, SQUARE_BUFFERS * S], F32, "squares", tag="w2_bf16_11")
+        bias2 = tile([P, len(row_tiles)], F32, "bias2")
+        top = tile([P, len(row_tiles)], F32, "top")
 
         def square_of(s):
-            return sines[s][:] if s < SQUARES_ON_SCALAR else squares[:, S * (s % 4) : S * (s % 4 + 1)]
+            place = s % SQUARE_BUFFERS
+            return sines[s][:] if s < SQUARES_ON_SCALAR else squares[:, S * place : S * (place + 1)]
 
         def sine_stage(s):
-            b, i = tiles[s]
-            for half in range(2):
-                cols = slice(BANK * half, BANK * (half + 1))
-                x2 = bank([P, BANK], "x2", "x2")
+            b, i = row_tiles[s]
+            for first in range(0, S, BANK):
+                cols = slice(first, first + BANK)
+                x2 = bank([P, BANK], "x2", "low")
                 for a in range(PASSES):
                     nc.tensor.matmul_mx(
                         out=x2[:],
@@ -204,13 +210,12 @@ def tile_list_electrolyte_recipe_picker_kernel(
                 nc.scalar.activation(square_of(s), sines[s][:], ACT.Square)
 
         def product_stage(s):
-            b, i = tiles[s]
             squared = square_of(s)
             if s >= SQUARES_ON_SCALAR:
                 nc.gpsimd.tensor_tensor(squared, sines[s][:], sines[s][:], ALU.mult)
-            for half in range(2):
-                cols = slice(BANK * half, BANK * (half + 1))
-                x1 = bank([P, BANK], "x1", "x1")
+            for first in range(0, S, BANK):
+                cols = slice(first, first + BANK)
+                x1 = bank([P, BANK], "x1", "high")
                 for a in range(PASSES):
                     nc.tensor.matmul_mx(
                         out=x1[:],
@@ -224,23 +229,34 @@ def tile_list_electrolyte_recipe_picker_kernel(
                 nc.vector.scalar_tensor_tensor(h[s][:, cols], squared[:, cols], 0.5, x1[:], ALU.subtract, ALU.mult)
             nc.vector.tensor_scalar(h[s][:], h[s][:], 2.0, None, ALU.mult, ALU.max, accum_out=top[:, s : s + 1])
 
-        rows_ps = ps.tile([P, SLOTS, P], F32, name="rows_ps", tag="bank_7")
-        for i in range(SLOTS):
+        for s in range(PACK // 2):
+            sine_stage(s)
+        rows_dealt = tile([P, PACK, P], F32, "rows_dealt", tag="w2_bf16_10")
+        nc.scalar.copy(
+            out=rows_dealt[:].rearrange("v i (q u) -> v i q u", u=RUN),
+            in_=rows_raw[:].rearrange("v (q i u) -> v i q u", i=PACK, u=RUN),
+        )
+        rows_ps = bank([P, PACK, P], "rows_ps", "low")
+        for i in range(PACK):
             nc.tensor.transpose(rows_ps[:, i, :], rows_dealt[:, i, :], identity[:])
         nc.scalar.copy(
-            rows[:].rearrange("p (c i) -> p c i", i=SLOTS), rows_ps[:, :, 0:10].rearrange("p i c -> p c i")
+            rows[:].rearrange("p (c i) -> p c i", i=PACK),
+            rows_ps[:, :, 0 : ROW_VECTORS * PASSES].rearrange("p i c -> p c i"),
         )
-        minus_temp2 = tile([P, len(tiles)], F32, "minus_temp2")
-        nc.scalar.activation(minus_temp2[:], row_values(TEMP2, 0, 0, len(tiles)), ACT.Copy, scale=-1.0)
-        for s in range(len(tiles)):
+        minus_temp2 = tile([P, len(row_tiles)], F32, "minus_temp2")
+        nc.scalar.activation(minus_temp2[:], row_values(TEMP2, 0, 0, len(row_tiles)), ACT.Copy, scale=-1.0)
+        for s in range(PACK // 2, PACK):
             sine_stage(s)
-        for s in range(len(tiles)):
+        product_stage(0)
+        for s in range(PACK, len(row_tiles)):
+            sine_stage(s)
+        for s in range(1, len(row_tiles)):
             product_stage(s)
 
-        look1 = [tile([P, SLOTS, M], F32, "look1_%d" % b, tag="codes_a_%d" % (1 - b)) for b in range(PASSES)]
-        look2 = [tile([P, SLOTS, M], F32, "look2_%d" % b, tag="scales_c_%d" % (1 - b)) for b in range(PASSES)]
-        z = tile([P, PASSES, SLOTS, M], F32, "z", tag="w2_bf16_11")
-        for s, (b, i) in enumerate(tiles):
+        look1 = [tile([P, PACK, M], F32, "look1_%d" % b, tag="w2_codes_%d" % (1 - b)) for b in range(PASSES)]
+        look2 = [tile([P, PACK, M], F32, "look2_%d" % b, tag="w2_scales_%d" % (1 - b)) for b in range(PASSES)]
+        z = tile([P, PASSES, PACK, M], F32, "z", tag="w2_bf16_11")
+        for s, (b, i) in enumerate(row_tiles):
             nc.scalar.activation(bias2[:, s : s + 1], top[:, s : s + 1], ACT.Copy, scale=minus_temp2[:, s : s + 1])
             nc.scalar.activation(
                 look1[b][:, i, :], h[s][:].indirect(pos1_sb[:]), ACT.Exp,
@@ -256,67 +272,67 @@ def tile_list_electrolyte_recipe_picker_kernel(
 
         w3_codes = tile([P, PASSES, N], U32, "w3_codes", tag="w2_bf16_01")
         w3_scales = tile([P, PASSES, N], U8, "w3_scales")
-        w3_rounded = tile([P, PASSES * N * SLOTS], BF16, "w3_bf16", tag="w_raw")
+        w3_rounded = tile([P, PASSES * N * PACK], BF16, "w3_bf16", tag="stage_3")
         for b in range(PASSES):
-            rounded = w3_rounded[:, N * SLOTS * b : N * SLOTS * (b + 1)]
+            rounded = w3_rounded[:, N * PACK * b : N * PACK * (b + 1)]
+            raw = w3_raw[:, PACK * N * b : PACK * N * (b + 1)]
             for n0 in range(0, N, P):
                 nc.gpsimd.tensor_scalar(
-                    rounded.rearrange("p (n i) -> p n i", i=SLOTS)[:, n0 : n0 + P, :],
-                    w3_raw[:, SLOTS * N * b : SLOTS * N * (b + 1)].rearrange("p (i n) -> p n i", i=SLOTS)[:, n0 : n0 + P, :],
+                    rounded.rearrange("p (n i) -> p n i", i=PACK)[:, n0 : n0 + P, :],
+                    raw.rearrange("p (i n) -> p n i", i=PACK)[:, n0 : n0 + P, :],
                     1.0, 0.0, ALU.mult, ALU.add,
                 )
             nc.vector.quantize_mx(out=w3_codes[:, b, :].bitcast(FP8X4), scales=w3_scales[:, b, :], in_=rounded)
 
-        roots = tile([P, 2, SLOTS * 128], F32, "roots", tag="h_7")
-        y = tile([P, PASSES, SLOTS * M], BF16, "y")
+        roots = tile([P, PASSES, PACK * M_PIECE], F32, "roots", tag="sine_%d" % (len(row_tiles) - 1))
+        y = tile([P, PASSES, PACK * M], BF16, "y")
         y_codes = tile([P, PASSES, M], U32, "y_codes")
         y_scales = tile([P, PASSES, M], U8, "y_scales")
-        result = tile([P, N // P, M], F32, "result", tag="wide_1")
+        result = tile([P, N // P, M], F32, "result", tag="stage_1")
+        pieces = [slice(m0, m0 + M_PIECE) for m0 in range(0, M, M_PIECE)]
+        pairs = N // (2 * P)
 
-        def make_y(b, m0, m1):
-            root = roots[:, (PASSES * M_PIECES.index((m0, m1)) + b) % 2, 0 : SLOTS * (m1 - m0)].rearrange("p (m i) -> p m i", i=SLOTS)
-            nc.scalar.activation(root, z[:, b, :, m0:m1].rearrange("p i m -> p m i"), ACT.Sqrt)
+        def quantise_y(b, cols):
+            values = slice(PACK * cols.start, PACK * cols.stop)
+            root = roots[:, b, :].rearrange("p (m i) -> p m i", i=PACK)
+            nc.scalar.activation(root, z[:, b, :, cols].rearrange("p i m -> p m i"), ACT.Sqrt)
             nc.vector.tensor_tensor(
-                y[:, b, SLOTS * m0 : SLOTS * m1].rearrange("p (m i) -> p m i", i=SLOTS),
+                y[:, b, values].rearrange("p (m i) -> p m i", i=PACK),
                 root,
-                row_values(GAIN, b, 0, SLOTS).unsqueeze(1).to_broadcast([P, m1 - m0, SLOTS]),
+                row_values(GAIN, b, 0, PACK).unsqueeze(1).to_broadcast([P, M_PIECE, PACK]),
                 ALU.mult,
             )
-
-        def quantise_y(b, m0, m1):
             nc.vector.quantize_mx(
-                out=y_codes[:, b, m0:m1].bitcast(FP8X4),
-                scales=y_scales[:, b, m0:m1],
-                in_=y[:, b, SLOTS * m0 : SLOTS * m1],
+                out=y_codes[:, b, cols].bitcast(FP8X4), scales=y_scales[:, b, cols], in_=y[:, b, values]
             )
 
-        def last_product(acc, b, m0, m1):
-            for pair in range(2):
+        def last_product(acc, b, cols):
+            for pair in range(pairs):
                 for k in range(2):
                     n = 2 * pair + k
                     nc.tensor.matmul_mx(
                         out=acc[pair][:, k, :],
                         lhsT=w3_codes[:, b, P * n : P * (n + 1)].bitcast(FP8X4),
                         lhsT_scale=w3_scales[:, b, P * n : P * (n + 1)],
-                        rhs=y_codes[:, b, m0:m1].bitcast(FP8X4),
-                        rhs_scale=y_scales[:, b, m0:m1],
+                        rhs=y_codes[:, b, cols].bitcast(FP8X4),
+                        rhs_scale=y_scales[:, b, cols],
                         start=(b == 0 and k == 0),
                         stop=(b == PASSES - 1 and k == 1),
                     )
 
-        sums = {}
-        for m0, m1 in M_PIECES:
-            sums[m0] = [bank([P, 2, m1 - m0], "acc", ring) for ring in ("x2", "x1")]
+        sums = []
+        for cols in pieces:
+            acc = [bank([P, 2, M_PIECE], "acc", ring) for ring in ("low", "high")]
+            sums.append(acc)
             for b in range(PASSES):
-                make_y(b, m0, m1)
-                quantise_y(b, m0, m1)
-                last_product(sums[m0], b, m0, m1)
-        for m0, m1 in M_PIECES:
-            for pair in range(2):
-                rows_out = slice(2 * pair, 2 * pair + 2)
-                copy = nc.vector.tensor_copy if pair == 0 and m1 == M else nc.scalar.copy
-                copy(result[:, rows_out, m0:m1], sums[m0][pair][:])
+                quantise_y(b, cols)
+                last_product(acc, b, cols)
+        for cols, acc in zip(pieces, sums):
+            for pair in range(pairs):
+                out_tiles = slice(2 * pair, 2 * pair + 2)
+                copy = nc.vector.tensor_copy if pair == 0 and cols.stop == M else nc.scalar.copy
+                copy(result[:, out_tiles, cols], acc[pair][:])
                 nc.sync.dma_start(
-                    out=out[:, m0:m1].rearrange("(n p) m -> p n m", p=P)[:, rows_out, :],
-                    in_=result[:, rows_out, m0:m1],
+                    out=out[:, cols].rearrange("(n p) m -> p n m", p=P)[:, out_tiles, :],
+                    in_=result[:, out_tiles, cols],
                 )

import math
from contextlib import ExitStack

import concourse.mybir as mybir
from concourse.masks import make_identity

K, T, S, M, H, N = 1024, 2048, 1024, 512, 1024, 512
FLOPS = 2 * (2 * K * H * S + H * N * M)

F32 = mybir.dt.float32
BF16 = mybir.dt.bfloat16
I32 = mybir.dt.int32
U32 = mybir.dt.uint32
U16 = mybir.dt.uint16
U8 = mybir.dt.uint8
FP8X4 = mybir.dt.float8_e4m3fn_x4
FP4X4 = mybir.dt.float4_e2m1fn_x4
ACT = mybir.ActivationFunctionType
ALU = mybir.AluOpType

P = 128
PACK = 4
PASS = P * PACK
PASSES = 2
RUN = 8
QUADRANTS = 4
BANK = 512
BANKS = 8
LIST_COLUMN = 16
SQUARES_ON_SCALAR = 1
SQUARE_BUFFERS = 4
M_PIECE = 128
TEMP1, SHIFT1, TEMP2, LIFT, GAIN = range(5)
ROW_VECTORS = 5


def tile_list_electrolyte_recipe_picker_kernel(
    tc, tab_words, tab_scales, offs, pos1, pos2, w1_words, w1_scales,
    w2, temp1, shift1, temp2, lift, gain, w3, out
):
    nc = tc.nc
    with ExitStack() as ctx:
        lists = ctx.enter_context(tc.tile_pool(name="lists", bufs=1))
        sb = ctx.enter_context(tc.tile_pool(name="sb", bufs=1))
        ps = ctx.enter_context(tc.psum_pool(name="ps", bufs=1))

        taken = {"low": [], "high": []}

        def bank(shape, name, ring):
            count = len(taken[ring])
            half_of_banks = BANKS // 2
            first = {"low": 0, "high": half_of_banks}[ring]
            number = count if ring == "low" and count < BANKS else first + count % half_of_banks
            taken[ring].append(number)
            return ps.tile(shape, F32, name=name, tag="bank_%d" % number)

        def tile(shape, dtype, name, tag=None):
            return sb.tile(shape, dtype, name=name, tag=tag or name, align_bytes=64)

        offs_sb = lists.tile([P, S // LIST_COLUMN], U16, name="offs_sb")
        nc.sync.dma_start(offs_sb[:], offs)
        pos1_sb = lists.tile([P, M // LIST_COLUMN], U16, name="pos1_sb")
        nc.sync.dma_start(pos1_sb[:], pos1)
        pos2_sb = lists.tile([P, M // LIST_COLUMN], U16, name="pos2_sb")
        nc.sync.dma_start(pos2_sb[:], pos2)

        tab_words_sb = []
        for a in range(PASSES):
            words = tile([P, T], I32, "tab_words_%d" % a, tag="stage_%d" % a)
            nc.sync.dma_start(out=words[:], in_=tab_words[a].rearrange("p t i -> p (t i)").bitcast(I32))
            tab_words_sb.append(words)
        tab_scales_sb = tile([P, T], U8, "tab_scales_sb", tag="stage_2")
        nc.gpsimd.memset(tab_scales_sb[:].bitcast(I32), 0)
        for quad in range(QUADRANTS):
            nc.sync.dma_start(
                out=tab_scales_sb[32 * quad : 32 * quad + 8, :].bitcast(I32),
                in_=tab_scales[:, 4 * quad : 4 * quad + 4, :].bitcast(I32),
            )
        one = tile([P, 1], F32, "one", tag="stage_3")
        nc.gpsimd.memset(one[:], 1.0)
        quarter_pi = tile([P, 1], F32, "quarter_pi")
        nc.vector.tensor_scalar(quarter_pi[:], one[:], math.pi / 4, None, ALU.mult)

        w2_raw = {}

        def load_w2(a, b, raw):
            nc.sync.dma_start(
                out=raw.rearrange("p (j c) -> p j c", j=PACK),
                in_=w2[PASS * a : PASS * (a + 1), PASS * b : PASS * (b + 1)].rearrange("(p j) c -> p j c", j=PACK),
            )
            w2_raw[a, b] = raw

        w2_first = tile([P, PASSES * PACK * PASS], F32, "w2_first", tag="stage_3")
        for a in range(PASSES):
            load_w2(a, 0, w2_first[:, PACK * PASS * a : PACK * PASS * (a + 1)])

        w1_scales_raw = tile([P, PASSES, H], U8, "w1_scales_raw", tag="stage_4")
        nc.gpsimd.memset(w1_scales_raw[:].bitcast(I32), 0)
        for quad in range(QUADRANTS):
            nc.sync.dma_start(
                out=w1_scales_raw[32 * quad : 32 * quad + 4, :, :].bitcast(I32),
                in_=w1_scales[:, 4 * quad : 4 * quad + 4, :].rearrange("a r e -> r a e").bitcast(I32),
            )
        rows_raw = tile([P, PASS], F32, "rows_raw")
        nc.vector.memset(rows_raw[:], 0.0)
        for v, vec in enumerate((temp1, shift1, temp2, lift, gain)):
            nc.gpsimd.dma_start(
                out=rows_raw[PASSES * v : PASSES * (v + 1), :], in_=vec.rearrange("(b c) -> b c", b=PASSES)
            )
        identity = tile([P, P], F32, "identity")
        make_identity(nc, identity[:])
        v_scales_pass1 = tile([P, S], U8, "v_scales_pass1")
        nc.vector.memset(v_scales_pass1[:].bitcast(I32), 0)

        v_words = []
        for a in range(PASSES):
            picked = tile([P, S], U32, "v_words_%d" % a)
            nc.vector.tensor_copy(picked[:], tab_words_sb[a][:].bitcast(U32).indirect(offs_sb[:]))
            v_words.append(picked)
        v_scales = tile([P, S], U8, "v_scales")
        nc.vector.tensor_copy(v_scales[:], tab_scales_sb[:].indirect(offs_sb[:]))
        for quad in range(QUADRANTS):
            nc.sync.dma_start(
                out=v_scales_pass1[32 * quad : 32 * quad + 4, :].bitcast(I32),
                in_=v_scales[32 * quad + 4 : 32 * quad + 8, :].bitcast(I32),
            )
        w1_raw = tile([P, PASSES, 2 * H], U8, "w1_raw", tag="stage_1")
        nc.sync.dma_start(out=w1_raw[:].bitcast(I32), in_=w1_words.rearrange("a p e -> p a e").bitcast(I32))
        for a, stage in enumerate(("stage_0", "stage_2")):
            load_w2(a, 1, tile([P, PACK * PASS], F32, "w2_second_%d" % a, tag=stage)[:])

        w2_codes = [tile([P, PASSES, PASS], U32, "w2_codes_%d" % b) for b in range(PASSES)]
        w2_scales = [tile([P, PASSES, PASS], U8, "w2_scales_%d" % b) for b in range(PASSES)]

        def quantise_w2(a, b, tiles_on_scalar, tiles_at_once):
            rounded = tile([P, PACK, PASS], BF16, "w2_bf16_%d%d" % (a, b))
            for i in range(PACK):
                copy = nc.scalar.copy if i < tiles_on_scalar else nc.vector.tensor_copy
                copy(
                    out=rounded[:, i, :].rearrange("p (q u j) -> p q u j", u=RUN, j=PACK),
                    in_=w2_raw[a, b].rearrange("p (j q i u) -> p i q u j", j=PACK, i=PACK, u=RUN)[:, i],
                )
                if (i + 1) % tiles_at_once == 0:
                    first = i + 1 - tiles_at_once
                    cols = slice(P * first, P * (i + 1))
                    nc.vector.quantize_mx(
                        out=w2_codes[b][:, a, cols].bitcast(FP8X4),
                        scales=w2_scales[b][:, a, cols],
                        in_=rounded[:, first : i + 1, :].rearrange("p i c -> p (i c)"),
                    )

        quantise_w2(0, 0, 3, PACK)
        quantise_w2(1, 0, 0, 1)
        quantise_w2(0, 1, 0, PACK)
        quantise_w2(1, 1, 0, 2)

        w1_codes = tile([P, PASSES, 2 * H], U8, "w1_codes", tag="w2_bf16_01")
        nc.vector.tensor_copy(
            out=w1_codes[:].bitcast(I32).rearrange("p a (b i q w) -> p (a b) i q w", b=PASSES, i=PACK, w=4),
            in_=w1_raw[:].bitcast(I32).rearrange("p a (b q i w) -> p (a b) i q w", b=PASSES, i=PACK, w=4),
        )
        w1_planes = tile([P, PASSES, H], U8, "w1_planes", tag="stage_0")
        nc.vector.tensor_copy(
            out=w1_planes[:].bitcast(I32).rearrange("p a (b i q w) -> p (a b) i q w", b=PASSES, i=PACK, w=2),
            in_=w1_scales_raw[:].bitcast(I32).rearrange("p a (b q i w) -> p (a b) i q w", b=PASSES, i=PACK, w=2),
        )

        rows = tile([P, ROW_VECTORS * PASSES * PACK], F32, "rows")

        def row_values(v, b, first, count=1):
            col = PACK * (PASSES * v + b) + first
            return rows[:, col : col + count]

        w3_raw = tile([P, PASSES * PACK * N], F32, "w3_raw", tag="stage_4")
        for b in range(PASSES):
            for i in range(PACK):
                nc.sync.dma_start(
                    out=w3_raw[:, N * (PACK * b + i) : N * (PACK * b + i + 1)],
                    in_=w3[PASS * b : PASS * (b + 1), :].rearrange("(q i u) n -> i q u n", i=PACK, u=RUN)[i],
                )

        row_tiles = [(b, i) for b in range(PASSES) for i in range(PACK)]
        sines = [tile([P, S], F32, "sine_%d" % s) for s in range(len(row_tiles))]
        h = [tile([P, S], F32, "h_first", tag="stage_2")] + sines[1:]
        squares = tile([P, SQUARE_BUFFERS * S], F32, "squares", tag="w2_bf16_11")
        bias2 = tile([P, len(row_tiles)], F32, "bias2")
        top = tile([P, len(row_tiles)], F32, "top")

        def square_of(s):
            place = s % SQUARE_BUFFERS
            return sines[s][:] if s < SQUARES_ON_SCALAR else squares[:, S * place : S * (place + 1)]

        def sine_stage(s):
            b, i = row_tiles[s]
            for first in range(0, S, BANK):
                cols = slice(first, first + BANK)
                x2 = bank([P, BANK], "x2", "low")
                for a in range(PASSES):
                    nc.tensor.matmul_mx(
                        out=x2[:],
                        lhsT=w2_codes[b][:, a, P * i : P * (i + 1)].bitcast(FP8X4),
                        lhsT_scale=w2_scales[b][:, a, P * i : P * (i + 1)],
                        rhs=v_words[a][:, cols].bitcast(FP8X4),
                        rhs_scale=v_scales[4 * a : P, cols],
                        start=(a == 0),
                        stop=(a == PASSES - 1),
                    )
                nc.scalar.activation(sines[s][:, cols], x2[:], ACT.Sin, bias=quarter_pi[:], scale=0.5)
            if s < SQUARES_ON_SCALAR:
                nc.scalar.activation(square_of(s), sines[s][:], ACT.Square)

        def product_stage(s):
            squared = square_of(s)
            if s >= SQUARES_ON_SCALAR:
                nc.gpsimd.tensor_tensor(squared, sines[s][:], sines[s][:], ALU.mult)
            for first in range(0, S, BANK):
                cols = slice(first, first + BANK)
                x1 = bank([P, BANK], "x1", "high")
                for a in range(PASSES):
                    nc.tensor.matmul_mx(
                        out=x1[:],
                        lhsT=w1_codes[:, a, 2 * P * s : 2 * P * (s + 1)].bitcast(FP4X4),
                        lhsT_scale=w1_planes[:, a, P * s : P * (s + 1)],
                        rhs=v_words[a][:, cols].bitcast(FP8X4),
                        rhs_scale=(v_scales, v_scales_pass1)[a][:, cols],
                        start=(a == 0),
                        stop=(a == PASSES - 1),
                    )
                nc.vector.scalar_tensor_tensor(h[s][:, cols], squared[:, cols], 0.5, x1[:], ALU.subtract, ALU.mult)
            nc.vector.tensor_scalar(h[s][:], h[s][:], 2.0, None, ALU.mult, ALU.max, accum_out=top[:, s : s + 1])

        for s in range(PACK // 2):
            sine_stage(s)
        rows_dealt = tile([P, PACK, P], F32, "rows_dealt", tag="w2_bf16_10")
        nc.scalar.copy(
            out=rows_dealt[:].rearrange("v i (q u) -> v i q u", u=RUN),
            in_=rows_raw[:].rearrange("v (q i u) -> v i q u", i=PACK, u=RUN),
        )
        rows_ps = bank([P, PACK, P], "rows_ps", "low")
        for i in range(PACK):
            nc.tensor.transpose(rows_ps[:, i, :], rows_dealt[:, i, :], identity[:])
        nc.scalar.copy(
            rows[:].rearrange("p (c i) -> p c i", i=PACK),
            rows_ps[:, :, 0 : ROW_VECTORS * PASSES].rearrange("p i c -> p c i"),
        )
        minus_temp2 = tile([P, len(row_tiles)], F32, "minus_temp2")
        nc.scalar.activation(minus_temp2[:], row_values(TEMP2, 0, 0, len(row_tiles)), ACT.Copy, scale=-1.0)
        for s in range(PACK // 2, PACK):
            sine_stage(s)
        product_stage(0)
        for s in range(PACK, len(row_tiles)):
            sine_stage(s)
        for s in range(1, len(row_tiles)):
            product_stage(s)

        look1 = [tile([P, PACK, M], F32, "look1_%d" % b, tag="w2_codes_%d" % (1 - b)) for b in range(PASSES)]
        look2 = [tile([P, PACK, M], F32, "look2_%d" % b, tag="w2_scales_%d" % (1 - b)) for b in range(PASSES)]
        z = tile([P, PASSES, PACK, M], F32, "z", tag="w2_bf16_11")
        for s, (b, i) in enumerate(row_tiles):
            nc.scalar.activation(bias2[:, s : s + 1], top[:, s : s + 1], ACT.Copy, scale=minus_temp2[:, s : s + 1])
            nc.scalar.activation(
                look1[b][:, i, :], h[s][:].indirect(pos1_sb[:]), ACT.Exp,
                bias=row_values(SHIFT1, b, i), scale=row_values(TEMP1, b, i),
            )
            nc.scalar.activation(
                look2[b][:, i, :], h[s][:].indirect(pos2_sb[:]), ACT.Exp,
                bias=bias2[:, s : s + 1], scale=row_values(TEMP2, b, i),
            )
            nc.vector.scalar_tensor_tensor(
                z[:, b, i, :], look2[b][:, i, :], row_values(LIFT, b, i), look1[b][:, i, :], ALU.mult, ALU.add
            )

        w3_codes = tile([P, PASSES, N], U32, "w3_codes", tag="w2_bf16_01")
        w3_scales = tile([P, PASSES, N], U8, "w3_scales")
        w3_rounded = tile([P, PASSES * N * PACK], BF16, "w3_bf16", tag="stage_3")
        for b in range(PASSES):
            rounded = w3_rounded[:, N * PACK * b : N * PACK * (b + 1)]
            raw = w3_raw[:, PACK * N * b : PACK * N * (b + 1)]
            for n0 in range(0, N, P):
                nc.gpsimd.tensor_scalar(
                    rounded.rearrange("p (n i) -> p n i", i=PACK)[:, n0 : n0 + P, :],
                    raw.rearrange("p (i n) -> p n i", i=PACK)[:, n0 : n0 + P, :],
                    1.0, 0.0, ALU.mult, ALU.add,
                )
            nc.vector.quantize_mx(out=w3_codes[:, b, :].bitcast(FP8X4), scales=w3_scales[:, b, :], in_=rounded)

        roots = tile([P, PASSES, PACK * M_PIECE], F32, "roots", tag="sine_%d" % (len(row_tiles) - 1))
        y = tile([P, PASSES, PACK * M], BF16, "y")
        y_codes = tile([P, PASSES, M], U32, "y_codes")
        y_scales = tile([P, PASSES, M], U8, "y_scales")
        result = tile([P, N // P, M], F32, "result", tag="stage_1")
        pieces = [slice(m0, m0 + M_PIECE) for m0 in range(0, M, M_PIECE)]
        pairs = N // (2 * P)

        def quantise_y(b, cols):
            values = slice(PACK * cols.start, PACK * cols.stop)
            root = roots[:, b, :].rearrange("p (m i) -> p m i", i=PACK)
            nc.scalar.activation(root, z[:, b, :, cols].rearrange("p i m -> p m i"), ACT.Sqrt)
            nc.vector.tensor_tensor(
                y[:, b, values].rearrange("p (m i) -> p m i", i=PACK),
                root,
                row_values(GAIN, b, 0, PACK).unsqueeze(1).to_broadcast([P, M_PIECE, PACK]),
                ALU.mult,
            )
            nc.vector.quantize_mx(
                out=y_codes[:, b, cols].bitcast(FP8X4), scales=y_scales[:, b, cols], in_=y[:, b, values]
            )

        def last_product(acc, b, cols):
            for pair in range(pairs):
                for k in range(2):
                    n = 2 * pair + k
                    nc.tensor.matmul_mx(
                        out=acc[pair][:, k, :],
                        lhsT=w3_codes[:, b, P * n : P * (n + 1)].bitcast(FP8X4),
                        lhsT_scale=w3_scales[:, b, P * n : P * (n + 1)],
                        rhs=y_codes[:, b, cols].bitcast(FP8X4),
                        rhs_scale=y_scales[:, b, cols],
                        start=(b == 0 and k == 0),
                        stop=(b == PASSES - 1 and k == 1),
                    )

        sums = []
        for cols in pieces:
            acc = [bank([P, 2, M_PIECE], "acc", ring) for ring in ("low", "high")]
            sums.append(acc)
            for b in range(PASSES):
                quantise_y(b, cols)
                last_product(acc, b, cols)
        for cols, acc in zip(pieces, sums):
            for pair in range(pairs):
                out_tiles = slice(2 * pair, 2 * pair + 2)
                copy = nc.vector.tensor_copy if pair == 0 and cols.stop == M else nc.scalar.copy
                copy(result[:, out_tiles, cols], acc[pair][:])
                nc.sync.dma_start(
                    out=out[:, cols].rearrange("(n p) m -> p n m", p=P)[:, out_tiles, :],
                    in_=result[:, out_tiles, cols],
                )
